import numpy as np
import ml_dtypes


def mxq(x, axis, fmt="e4m3"):
    dtype, down = {"e4m3": (ml_dtypes.float8_e4m3fn, 7), "e5m2": (ml_dtypes.float8_e5m2, 14)}[fmt]
    v = np.moveaxis(np.asarray(x, np.float32).astype(ml_dtypes.bfloat16).astype(np.float64), axis, -1)
    blocks = v.reshape(v.shape[:-1] + (-1, 32))
    amax = np.abs(blocks).max(-1, keepdims=True)
    byte = np.maximum(np.where(amax > 0, np.frexp(amax)[1] - 1 + 127, 0) - down, 1)
    scale = np.exp2(byte - 127.0)
    codes = (blocks / scale).astype(np.float32).astype(dtype).astype(np.float64)
    return np.moveaxis((codes * scale).reshape(v.shape), -1, axis)


WIDE = False


def mx_kscale(k):
    if not WIDE:
        return np.ones(k)
    levels = np.array([10, -10, 5, -5, 0])
    if k % 512:
        return np.exp2(np.random.permutation(np.resize(levels, k // 32))).repeat(32)
    a = np.empty((k // 512, 16))
    for p in range(k // 512):
        a[p, :8] = np.random.permutation(np.resize(levels, 8))
        for g in range(8):
            far = levels[np.abs(levels - a[p, g]) >= 10]
            a[p, g + 8] = far[np.random.randint(len(far))]
    return np.exp2(a.ravel()).repeat(32)


BF16 = ml_dtypes.bfloat16


def bf(x):
    return np.asarray(x, np.float32).astype(BF16)


def f64(x):
    return np.asarray(x).astype(np.float64)

def planes(Y):
    n, m = Y.shape
    b = f64(bf(Y)).reshape(n // 32, 32, m)
    amax = np.abs(b).max(1)
    byte = np.clip(np.where(amax > 0, np.frexp(amax)[1] - 1 + 127 - 7, 1), 1, 254)
    codes = (b * np.exp2(127.0 - byte)[:, None, :]).reshape(n, m).astype(np.float32).astype(ml_dtypes.float8_e4m3fn).view(np.uint8)
    words = codes.reshape(n // 512, 128, 4, m).transpose(0, 1, 3, 2)
    return np.ascontiguousarray(words), np.ascontiguousarray(byte.astype(np.uint8).reshape(n // 512, 16, m))


S, T, C, H, D = 1024, 1024, 512, 4, 512


def setup_inputs():
    s, t = mx_kscale(C), mx_kscale(D)
    c = np.random.standard_normal((S, C)) * s
    wq = np.random.standard_normal((C, H, D)) / np.sqrt(C) / s[:, None, None] * t
    k = np.random.standard_normal((T, D)) * (0.5 + np.random.random((T, 1))) + 0.5 * np.random.standard_normal((T, 1))
    kg = (1.0 + 0.1 * np.random.standard_normal(D)) / t
    kb = 0.3 * np.random.standard_normal(D) / t
    w = np.random.standard_normal((S, H))
    return {"c": bf(c), "wq": bf(wq), "k": bf(k), "kg": bf(kg), "kb": bf(kb), "w": bf(w)}


def normalize_keys(k, kg, kb):
    mu = np.mean(k, axis=-1, keepdims=True)
    centered = k - mu
    var = np.mean(centered * centered, axis=-1, keepdims=True)
    return centered / np.sqrt(var + 1e-6) * kg + kb


def core(c, wq, k, kg, kb, w):
    q = mxq(f64(c), 1, "e4m3") @ mxq(f64(wq).transpose(1, 0, 2), 1, "e4m3")
    kn = normalize_keys(f64(k), f64(kg), f64(kb))
    logits = (mxq(q, 2, "e4m3") @ mxq(kn, 1, "e4m3").T) / np.sqrt(D)
    r = np.maximum(logits, 0.0)
    return np.sum(f64(w).T[:, :, None] * r, axis=0)


def reference(c, wq, k, kg, kb, w):
    R_out = core(c, wq, k, kg, kb, w)
    words, scales = planes(R_out)
    return R_out, words, scales

@@ -1,0 +1,460 @@
+from contextlib import ExitStack
+import math
+
+import concourse.mybir as mybir
+from concourse.masks import make_identity
+
+S, T, C, H, D = 1024, 1024, 512, 4, 512
+FLOPS = 2 * S * C * H * D + 2 * H * S * T * D
+
+F32 = mybir.dt.float32
+BF16 = mybir.dt.bfloat16
+U32 = mybir.dt.uint32
+I32 = mybir.dt.int32
+U8 = mybir.dt.uint8
+FP8X4 = mybir.dt.float8_e4m3fn_x4
+ALU = mybir.AluOpType
+ACT = mybir.ActivationFunctionType
+
+P = 128
+PACK = 4
+BANK = 512
+EPS = 1e-6
+
+
+def tile_lightningindexerheadweightedreluscore_x1_kernel(tc, c, wq, k, kg, kb, w, out_0, out_1, out_2):
+    nc = tc.nc
+    with ExitStack() as ctx:
+        keep = ctx.enter_context(tc.tile_pool(name="keep", bufs=1))
+        work = ctx.enter_context(tc.tile_pool(name="work", bufs=2))
+        psum = ctx.enter_context(tc.psum_pool(name="psum", bufs=2))
+        ctx.enter_context(tc.manual_schedule())
+
+        def bank_a():
+            return psum.tile([P, BANK], F32, name="bank_a", bufs=4)
+
+        def bank_v():
+            return psum.tile([P, BANK], F32, name="bank_v", bufs=4)
+
+        key_groups = [(0, 2), (2, 2), (4, 4)]
+        k_sb, c_sb, wq_sb = {}, {}, {}
+
+        def load_k(first, count):
+            t = keep.tile([P, count, D], BF16, name="k_sb%d" % first)
+            nc.sync.dma_start(out=t[:], in_=k[first * P:(first + count) * P, :].rearrange("(n p) d -> p n d", p=P))
+            for n in range(count):
+                k_sb[first + n] = t[:, n, :]
+
+        def load_c(g):
+            c_sb[g] = keep.tile([P, PACK, C], BF16, name="c_sb%d" % g)
+            nc.sync.dma_start(out=c_sb[g][:], in_=c[g * BANK:(g + 1) * BANK, :].rearrange("(p j) i -> p j i", j=PACK))
+
+        def load_wq(h):
+            wq_sb[h] = keep.tile([P, PACK, D], BF16, name="wq_sb%d" % h)
+            nc.sync.dma_start(out=wq_sb[h][:], in_=wq[:, h, :].rearrange("(p i) d -> p i d", i=PACK))
+
+        w_sb = keep.tile([P, 2, PACK * H], BF16, name="w_sb")
+        kg_sb = keep.tile([P, PACK], BF16, name="kg_sb")
+        kb_sb = keep.tile([P, PACK], BF16, name="kb_sb")
+        load_k(*key_groups[0])
+        nc.scalar.dma_start(out=w_sb[:], in_=w.rearrange("(g p j) h -> p g (j h)", g=2, j=PACK))
+        nc.scalar.dma_start(out=kg_sb[:], in_=kg.rearrange("(p j) -> p j", j=PACK))
+        nc.scalar.dma_start(out=kb_sb[:], in_=kb.rearrange("(p j) -> p j", j=PACK))
+        load_wq(0)
+        load_k(*key_groups[1])
+        load_c(0)
+        load_k(*key_groups[2])
+        load_wq(1)
+        load_wq(2)
+        load_c(1)
+        load_wq(3)
+
+        ident = keep.tile([P, P], F32, name="ident")
+        make_identity(nc, ident[:])
+        w_col = keep.tile([P, 2, PACK * H], F32, name="w_col")
+        kg_col = keep.tile([P, PACK], F32, name="kg_col")
+        kb_col = keep.tile([P, PACK], F32, name="kb_col")
+
+        def constants():
+            nc.gpsimd.tensor_scalar(w_col[:], w_sb[:], 1.0 / math.sqrt(D), 1.0, ALU.mult, ALU.mult)
+            nc.gpsimd.tensor_scalar(kg_col[:], kg_sb[:], 1.0, 1.0, ALU.mult, ALU.mult)
+            nc.gpsimd.tensor_scalar(kb_col[:], kb_sb[:], 1.0, 1.0, ALU.mult, ALU.mult)
+
+        def planes(name, width):
+            codes = keep.tile([P, width], U32, name=name + "_codes", align_bytes=64)
+            scales = keep.tile([P, width], U8, name=name + "_scales", align_bytes=64)
+            return codes, scales
+
+        def quantize(dst, cols, src):
+            nc.vector.quantize_mx(out=dst[0][:, cols].bitcast(FP8X4), scales=dst[1][:, cols], in_=src)
+
+        def mx(out, lhs, lcols, rhs, rcols):
+            nc.tensor.matmul_mx(out=out, lhsT=lhs[0][:, lcols].bitcast(FP8X4), lhsT_scale=lhs[1][:, lcols],
+                                rhs=rhs[0][:, rcols].bitcast(FP8X4), rhs_scale=rhs[1][:, rcols], start=True, stop=True)
+
+        def blk(n, width=P):
+            return slice(n * width, (n + 1) * width)
+
+        def pool_copy(out, in_):
+            nc.gpsimd.tensor_scalar(out, in_, 1.0, 1.0, ALU.mult, ALU.mult)
+
+        def vec_copy(out, in_):
+            nc.vector.tensor_copy(out=out, in_=in_)
+
+        def act_copy(out, in_):
+            nc.scalar.copy(out=out, in_=in_)
+
+        kn_mx = planes("kn", T)
+        stats, mean_var, rstd, neg_mean, z, kn_slots, kn_words = {}, {}, {}, {}, {}, {}, {}
+
+        def key_stats(tt):
+            stats[tt] = keep.tile([P, 6], F32, name="stats%d" % tt)
+            nc.vector.bn_stats(stats[tt][:], k_sb[tt])
+
+        def key_aggr(first, count):
+            mean_var[first] = keep.tile([P, count, 2], F32, name="mean_var%d" % first)
+            for n in range(count):
+                nc.vector.bn_aggr(mean_var[first][:, n, :], stats[first + n][:])
+
+        def key_rstd(first, count):
+            rstd[first] = keep.tile([P, count], F32, name="rstd%d" % first)
+            nc.scalar.activation(rstd[first][:], mean_var[first][:, :, 1], ACT.Abs_reciprocal_sqrt, bias=EPS)
+
+        def key_center(first, count):
+            for n in range(count):
+                z[first + n] = work.tile([P, PACK, P], F32, name="z", bufs=4)
+                nc.vector.tensor_scalar(z[first + n][:], k_sb[first + n].rearrange("t (p j) -> t j p", j=PACK),
+                                        mean_var[first][:, n, 0:1], rstd[first][:, n:n + 1], ALU.subtract, ALU.mult)
+
+        def key_center_pool(first, count):
+            neg_mean[first] = keep.tile([P, count], F32, name="neg_mean%d" % first)
+            nc.gpsimd.tensor_scalar(neg_mean[first][:], mean_var[first][:, :, 0], -1.0, 1.0, ALU.mult, ALU.mult)
+            for n in range(count):
+                z[first + n] = work.tile([P, PACK, P], F32, name="z", bufs=4)
+                nc.gpsimd.tensor_scalar(z[first + n][:], k_sb[first + n].rearrange("t (p j) -> t j p", j=PACK),
+                                        neg_mean[first][:, n:n + 1], rstd[first][:, n:n + 1], ALU.add, ALU.mult)
+
+        def key_center_act(first, count):
+            neg_mean[first] = keep.tile([P, count], F32, name="neg_mean%d" % first)
+            nc.vector.scalar_tensor_tensor(neg_mean[first][:], mean_var[first][:, :, 0], -1.0, rstd[first][:], ALU.mult, ALU.mult)
+            for n in range(count):
+                z[first + n] = work.tile([P, PACK, P], F32, name="z", bufs=4)
+                nc.scalar.activation(z[first + n][:], k_sb[first + n].rearrange("t (p j) -> t j p", j=PACK), ACT.Identity,
+                                     bias=neg_mean[first][:, n:n + 1], scale=rstd[first][:, n:n + 1])
+
+        key_bank = {}
+
+        def keys_out(th):
+            kn_slots[th] = work.tile([P, PACK, BANK], BF16, name="kn_slots", bufs=1)
+            for j in range(PACK):
+                bank = bank_a()
+                for n in range(4):
+                    nc.tensor.transpose(bank[:, blk(n)], z[4 * th + n][:, j, :], ident[:])
+                nc.scalar.activation(kn_slots[th][:, j, :], bank[:], ACT.Identity,
+                                     bias=kb_col[:, j:j + 1], scale=kg_col[:, j:j + 1])
+
+        def key_pack(th, copy):
+            kn_words[th] = work.tile([P, BANK, PACK], BF16, name="kn_words", bufs=1, align_bytes=64)
+            copy(kn_words[th][:], kn_slots[th][:].rearrange("p j t -> p t j"))
+
+        def key_quant(th):
+            quantize(kn_mx, blk(th, BANK), kn_words[th][:].rearrange("p t j -> p (t j)"))
+
+        c_mx, c_words, c_bank, wq_mx, wq_words = {}, {}, {}, {}, {}
+
+        def c_turn(g, b):
+            words = c_sb[g][:].rearrange("p j i -> p (j i)").bitcast(F32)
+            bank = bank_a()
+            c_bank[g, b] = bank
+            for jj in range(2):
+                j = 2 * b + jj
+                for u in range(2):
+                    nc.tensor.transpose(bank[:, blk(2 * jj + u)], words[:, j * 256 + u:(j + 1) * 256:2], ident[:])
+
+        def c_out(g, b):
+            if b == 0:
+                c_words[g] = work.tile([P, BANK * PACK], BF16, name="c_words", bufs=1, align_bytes=64)
+            dst = c_words[g][:, blk(b, 1024)].bitcast(F32).rearrange("p (jj r u) -> p jj r u", jj=2, u=2)
+            nc.scalar.copy(out=dst, in_=c_bank[g, b][:].rearrange("p (jj u r) -> p jj r u", jj=2, u=2))
+
+        def c_quant(g):
+            c_mx[g] = planes("c%d" % g, BANK)
+            quantize(c_mx[g], slice(0, BANK), c_words[g][:])
+
+        def wq_pack(h, first, count, copy, tag):
+            wq_words[h, first] = work.tile([P, count, P, PACK], BF16, name=tag, bufs=1, align_bytes=64)
+            copy(wq_words[h, first][:], wq_sb[h][:].rearrange("p i (m j) -> p j m i", j=PACK)[:, first:first + count, :, :])
+
+        def wq_quant(h, first, count):
+            if h not in wq_mx:
+                wq_mx[h] = planes("wq%d" % h, D)
+            quantize(wq_mx[h], slice(first * P, (first + count) * P), wq_words[h, first][:].rearrange("p j m i -> p (j m i)"))
+
+        q_mx, q_words, q_bank = {}, {}, {}
+
+        def q_mm(g, h, sj):
+            bank = bank_a()
+            q_bank[g, h, sj] = bank
+            for j in range(PACK):
+                mx(bank[:, blk(j)], wq_mx[h], blk(j), c_mx[g], blk(sj))
+
+        def q_out(g, h, sj, copy=act_copy):
+            if sj == 0:
+                q_words[g, h] = work.tile([P, BANK, PACK], BF16, name="q_words", bufs=3, align_bytes=64)
+                q_mx[g, h] = planes("q%d%d" % (g, h), BANK)
+            copy(q_words[g, h][:, blk(sj), :], q_bank[g, h, sj][:].rearrange("p (j n) -> p n j", j=PACK))
+
+        def q_quant(g, h, first=0, count=PACK):
+            cols = slice(first * P, (first + count) * P)
+            quantize(q_mx[g, h], cols, q_words[g, h][:, cols, :].rearrange("p s j -> p (s j)"))
+
+        w_row, w_bank = {}, {}
+
+        def w_turn(g, h):
+            bank = bank_a()
+            w_bank[g, h] = bank
+            for j in range(PACK):
+                col = w_col[:, g, j * H + h:j * H + h + 1]
+                nc.tensor.transpose(bank[:, blk(j)], col.to_broadcast([P, P]), ident[:])
+
+        def w_out(g, h):
+            w_row[g, h] = keep.tile([P, BANK], F32, name="w_row%d%d" % (g, h))
+            nc.scalar.copy(out=w_row[g, h][:], in_=w_bank[g, h][:])
+
+        t_bank, r_t, d_bank, relu_d, f_bank, part, res, res_words = {}, {}, {}, {}, {}, {}, {}, {}
+        res_codes, res_scales = {}, {}
+
+        def t_mm(su, n, h):
+            g, th = divmod(su, 2)
+            t_bank[su, n, h] = bank_v()
+            mx(t_bank[su, n, h][:], kn_mx, blk(4 * th + n), q_mx[g, h], slice(0, BANK))
+
+        def t_out(su, n, h):
+            r_t[su, n, h] = work.tile([P, BANK], F32, name="r_t", bufs=20)
+            nc.vector.scalar_tensor_tensor(r_t[su, n, h][:], t_bank[su, n, h][:], 0.0, w_row[su // 2, h][:], ALU.max, ALU.mult)
+
+        def d_mm(su, j, h):
+            g, th = divmod(su, 2)
+            d_bank[su, j, h] = bank_a()
+            mx(d_bank[su, j, h][:], q_mx[g, h], blk(j), kn_mx, blk(th, BANK))
+
+        def d_out(su, j, h):
+            relu_d[su, j, h] = work.tile([P, BANK], F32, name="relu_d", bufs=10)
+            nc.scalar.activation(relu_d[su, j, h][:], d_bank[su, j, h][:], ACT.Relu)
+
+        def f_turn(su, j):
+            f_bank[su, j] = bank_v()
+            for n in range(4):
+                for h in range(2):
+                    nc.tensor.matmul(f_bank[su, j][:, blk(n)], lhsT=r_t[su, n, h][:, blk(j)], rhs=ident[:],
+                                     start=(h == 0), stop=(h == 1), is_transpose=True)
+
+        def weight(su, j, h):
+            return w_col[:, su // 2, j * H + h:j * H + h + 1]
+
+        def f_first(su, j, cols=slice(0, BANK)):
+            if cols.start == 0:
+                part[su, j] = work.tile([P, BANK], F32, name="part", bufs=3)
+            nc.vector.scalar_tensor_tensor(part[su, j][:, cols], relu_d[su, j, 2][:, cols], weight(su, j, 2),
+                                           f_bank[su, j][:, cols], ALU.mult, ALU.add)
+
+        def f_second(su, j, cols=slice(0, BANK)):
+            g, th = divmod(su, 2)
+            if j == 0:
+                res[su] = work.tile([P, PACK, BANK], F32, name="res")
+            nc.vector.scalar_tensor_tensor(res[su][:, j, cols], relu_d[su, j, 3][:, cols], weight(su, j, 3),
+                                           part[su, j][:, cols], ALU.mult, ALU.add)
+            rows = out_0[blk(g, BANK), blk(th, BANK)].rearrange("(p j) t -> p j t", j=PACK)
+            nc.sync.dma_start(out=rows[:, j, cols], in_=res[su][:, j, cols])
+
+        def res_pack(su, first, count, copy, tag):
+            res_words[su, first] = work.tile([P, count * P, PACK], BF16, name=tag, bufs=2, align_bytes=64)
+            copy(res_words[su, first][:], res[su][:, :, first * P:(first + count) * P].rearrange("p j t -> p t j"))
+
+        def res_quant(su, first, count):
+            g, th = divmod(su, 2)
+            if su not in res_codes:
+                res_codes[su] = work.tile([P, BANK], U32, name="res_codes", align_bytes=64)
+            if g not in res_scales:
+                res_scales[g] = keep.tile([P, T], U8, name="res_scales%d" % g, align_bytes=64)
+            cols = slice(first * P, (first + count) * P)
+            nc.vector.quantize_mx(out=res_codes[su][:, cols].bitcast(FP8X4),
+                                  scales=res_scales[g][:, th * BANK + cols.start:th * BANK + cols.stop],
+                                  in_=res_words[su, first][:].rearrange("p t j -> p (t j)"))
+
+        def res_store(su):
+            g, th = divmod(su, 2)
+            dst = out_1[g].rearrange("p m t -> p (m t)").bitcast(I32)
+            nc.sync.dma_start(out=dst[:, blk(th, BANK)], in_=res_codes[su][:].bitcast(I32))
+            if th == 1:
+                for q in range(4):
+                    eng = nc.scalar if (g == 1 and q % 2 == 1) else nc.sync
+                    eng.dma_start(out=out_2[g, 4 * q:4 * q + 4, :].bitcast(I32),
+                                  in_=res_scales[g][32 * q:32 * q + 4, :].bitcast(I32))
+
+        g0, g1, g2 = key_groups
+
+        def queries(g, h):
+            for sj in range(PACK):
+                q_mm(g, h, sj)
+                q_out(g, h, sj)
+
+        def weights(g, h):
+            w_turn(g, h)
+            w_out(g, h)
+
+        def c_in(g):
+            for b in range(2):
+                c_turn(g, b)
+                c_out(g, b)
+
+        def t_mms(su, h, *ns):
+            for n in ns:
+                t_mm(su, n, h)
+
+        def t_outs(su, h, *ns):
+            for n in ns:
+                t_out(su, n, h)
+
+        key_stats(0)
+        key_stats(1)
+        constants()
+        key_aggr(*g0)
+        key_rstd(*g0)
+        wq_pack(0, 0, 2, pool_copy, "pool_words")
+        wq_pack(0, 2, 2, act_copy, "act_words")
+        key_stats(2)
+        key_stats(3)
+        key_aggr(*g1)
+        key_rstd(*g1)
+        key_center(*g0)
+        c_in(0)
+        wq_quant(0, 2, 2)
+        key_center(*g1)
+        key_stats(4)
+        c_quant(0)
+        wq_quant(0, 0, 2)
+        keys_out(0)
+        queries(0, 0)
+        wq_pack(1, 0, 2, pool_copy, "pool_words")
+        key_stats(5)
+        key_stats(6)
+        key_stats(7)
+        key_aggr(*g2)
+        key_rstd(*g2)
+        key_pack(0, vec_copy)
+        wq_pack(1, 2, 2, vec_copy, "act_words")
+        weights(0, 0)
+        c_in(1)
+        key_quant(0)
+        q_quant(0, 0)
+        t_mms(0, 0, 0, 1, 2, 3)
+        key_center(*g2)
+        keys_out(1)
+        wq_quant(1, 2, 2)
+        wq_quant(1, 0, 2)
+        wq_pack(2, 0, 3, pool_copy, "pool_words")
+        queries(0, 1)
+        weights(0, 1)
+        t_outs(0, 0, 0, 1, 2, 3)
+        c_quant(1)
+        queries(1, 0)
+        key_pack(1, vec_copy)
+        wq_pack(2, 3, 1, vec_copy, "act_words")
+        q_quant(0, 1)
+        t_mms(0, 1, 0, 1, 2, 3)
+        key_quant(1)
+        wq_quant(2, 3, 1)
+        wq_quant(2, 0, 3)
+        wq_pack(3, 0, 3, pool_copy, "pool_words")
+        weights(1, 0)
+        queries(0, 2)
+        t_outs(0, 1, 0, 1)
+        t_mms(1, 0, 0, 1)
+        t_outs(0, 1, 2, 3)
+        t_mms(1, 0, 2, 3)
+        wq_pack(3, 3, 1, vec_copy, "act_words")
+        wq_quant(3, 0, 3)
+        q_quant(1, 0)
+        wq_quant(3, 3, 1)
+        weights(1, 1)
+        q_mm(0, 3, 0)
+        q_out(0, 3, 0)
+        q_mm(0, 3, 1)
+        q_out(0, 3, 1)
+        t_outs(1, 0, 0, 1)
+        t_mms(1, 1, 0, 1)
+        q_quant(0, 2)
+        t_outs(1, 0, 2, 3)
+        q_quant(0, 3, 0, 2)
+
+        units = [(su, j) for su in range(4) for j in range(PACK)]
+        todo_t = [(su, n, h) for su, h in ((1, 1), (2, 0), (2, 1), (3, 0), (3, 1)) for n in range(4)][2:]
+        todo_q = [(0, 3, 2), (0, 3, 3)] + [(1, 1, sj) for sj in range(PACK)] + [(1, h, sj) for sj in range(PACK) for h in (2, 3)]
+
+        def unit_act(i):
+            su, j = units[i]
+            for h in (2, 3):
+                d_mm(su, j, h)
+                d_out(su, j, h)
+            for task in todo_q[2 * i:2 * i + 2]:
+                q_mm(*task)
+                q_out(*task)
+
+        def q_ready(i):
+            for g, h, sj in todo_q[2 * i:2 * i + 2]:
+                if h >= 2:
+                    q_quant(g, h, sj, 1)
+                elif sj == 3:
+                    q_quant(g, h)
+
+        t_count = [2, 2, 2, 0, 2, 2, 2, 2, 2, 1, 1, 0, 0, 0, 0, 0]
+        ahead = [1, 2, 3, 4, 5, 6, 7, 8, 9, 11, 13, 14, 15, 15, 15, 15]
+        f_turn(0, 0)
+        issued = 1
+        unit_act(0)
+        t_outs(1, 1, 0, 1)
+        done = 0
+        for i, (su, j) in enumerate(units[:-1]):
+            mine = todo_t[done:done + t_count[i]]
+            done = done + t_count[i]
+            for t in mine:
+                t_mm(*t)
+            while issued < min(16, ahead[i] + 1):
+                unit_act(issued)
+                issued = issued + 1
+            if mine:
+                t_out(*mine[0])
+            f_first(su, j)
+            if len(mine) > 1:
+                t_out(*mine[1])
+            f_turn(*units[i + 1])
+            if i > 0:
+                f_second(*units[i - 1])
+            q_ready(i)
+            if i in (7, 8, 9, 10):
+                res_quant(0, i - 7, 1)
+            if i == 10:
+                res_store(0)
+            if i in (5, 6, 7, 8):
+                res_pack(0, i - 5, 1, pool_copy, "pool_res")
+            if i in (9, 10, 13, 14):
+                res_pack((i - 5) // 4, 2 * ((i - 5) % 4), 2, act_copy, "act_res")
+            if i in (11, 12):
+                res_quant(1, 2 * (i - 11), 2)
+            if i == 12:
+                res_store(1)
+        halves = (slice(0, 256), slice(256, 512))
+        f_first(3, 3, halves[0])
+        f_second(3, 2)
+        f_first(3, 3, halves[1])
+        res_quant(2, 0, 2)
+        f_second(3, 3, halves[0])
+        res_pack(3, 0, 2, act_copy, "act_res")
+        res_quant(2, 2, 2)
+        res_store(2)
+        f_second(3, 3, halves[1])
+        res_pack(3, 2, 2, vec_copy, "pool_res")
+        res_quant(3, 0, 2)
+        res_quant(3, 2, 2)
+        res_store(3)

@@ -20,6 +20,7 @@ P = 128
 PACK = 4
 BANK = 512
 EPS = 1e-6
+RUN = 8
 
 
 def tile_lightningindexerheadweightedreluscore_x1_kernel(tc, c, wq, k, kg, kb, w, out_0, out_1, out_2):
@@ -50,16 +51,16 @@ def tile_lightningindexerheadweightedreluscore_x1_kernel(tc, c, wq, k, kg, kb, w
             nc.sync.dma_start(out=c_sb[g][:], in_=c[g * BANK:(g + 1) * BANK, :].rearrange("(p j) i -> p j i", j=PACK))
 
         def load_wq(h):
-            wq_sb[h] = keep.tile([P, PACK, D], BF16, name="wq_sb%d" % h)
+            wq_sb[h] = work.tile([P, PACK, D], BF16, name="wq_sb%d" % h, tag="wq_then_res", bufs=4)
             nc.sync.dma_start(out=wq_sb[h][:], in_=wq[:, h, :].rearrange("(p i) d -> p i d", i=PACK))
 
         w_sb = keep.tile([P, 2, PACK * H], BF16, name="w_sb")
-        kg_sb = keep.tile([P, PACK], BF16, name="kg_sb")
-        kb_sb = keep.tile([P, PACK], BF16, name="kb_sb")
+        gain_rows = keep.tile([2 * PACK, P], BF16, name="gain_rows")
         load_k(*key_groups[0])
         nc.scalar.dma_start(out=w_sb[:], in_=w.rearrange("(g p j) h -> p g (j h)", g=2, j=PACK))
-        nc.scalar.dma_start(out=kg_sb[:], in_=kg.rearrange("(p j) -> p j", j=PACK))
-        nc.scalar.dma_start(out=kb_sb[:], in_=kb.rearrange("(p j) -> p j", j=PACK))
+        for first, vec in ((0, kg), (PACK, kb)):
+            nc.scalar.dma_start(out=gain_rows[first:first + PACK, :].rearrange("j (q r) -> j q r", r=RUN),
+                                in_=vec.rearrange("(q j r) -> j q r", j=PACK, r=RUN))
         load_wq(0)
         load_k(*key_groups[1])
         load_c(0)
@@ -72,13 +73,18 @@ def tile_lightningindexerheadweightedreluscore_x1_kernel(tc, c, wq, k, kg, kb, w
         ident = keep.tile([P, P], F32, name="ident")
         make_identity(nc, ident[:])
         w_col = keep.tile([P, 2, PACK * H], F32, name="w_col")
-        kg_col = keep.tile([P, PACK], F32, name="kg_col")
-        kb_col = keep.tile([P, PACK], F32, name="kb_col")
+        gain_wide = keep.tile([P, P], F32, name="gain_wide")
+        gain_col = keep.tile([P, 2 * PACK], F32, name="gain_col")
+        nc.gpsimd.memset(gain_wide[:], 0.0)
 
         def constants():
             nc.gpsimd.tensor_scalar(w_col[:], w_sb[:], 1.0 / math.sqrt(D), 1.0, ALU.mult, ALU.mult)
-            nc.gpsimd.tensor_scalar(kg_col[:], kg_sb[:], 1.0, 1.0, ALU.mult, ALU.mult)
-            nc.gpsimd.tensor_scalar(kb_col[:], kb_sb[:], 1.0, 1.0, ALU.mult, ALU.mult)
+            nc.gpsimd.tensor_scalar(gain_wide[0:2 * PACK, :], gain_rows[:], 1.0, 1.0, ALU.mult, ALU.mult)
+
+        def gain_turn():
+            bank = bank_v()
+            nc.tensor.transpose(bank[:, 0:P], gain_wide[:], ident[:])
+            nc.scalar.copy(out=gain_col[:], in_=bank[:, 0:2 * PACK])
 
         def planes(name, width):
             codes = keep.tile([P, width], U32, name=name + "_codes", align_bytes=64)
@@ -123,7 +129,7 @@ def tile_lightningindexerheadweightedreluscore_x1_kernel(tc, c, wq, k, kg, kb, w
         def key_center(first, count):
             for n in range(count):
                 z[first + n] = work.tile([P, PACK, P], F32, name="z", bufs=4)
-                nc.vector.tensor_scalar(z[first + n][:], k_sb[first + n].rearrange("t (p j) -> t j p", j=PACK),
+                nc.vector.tensor_scalar(z[first + n][:].rearrange("t j (q r) -> t j q r", r=RUN), k_sb[first + n].rearrange("t (q j r) -> t j q r", j=PACK, r=RUN),
                                         mean_var[first][:, n, 0:1], rstd[first][:, n:n + 1], ALU.subtract, ALU.mult)
 
         def key_center_pool(first, count):
@@ -131,7 +137,7 @@ def tile_lightningindexerheadweightedreluscore_x1_kernel(tc, c, wq, k, kg, kb, w
             nc.gpsimd.tensor_scalar(neg_mean[first][:], mean_var[first][:, :, 0], -1.0, 1.0, ALU.mult, ALU.mult)
             for n in range(count):
                 z[first + n] = work.tile([P, PACK, P], F32, name="z", bufs=4)
-                nc.gpsimd.tensor_scalar(z[first + n][:], k_sb[first + n].rearrange("t (p j) -> t j p", j=PACK),
+                nc.gpsimd.tensor_scalar(z[first + n][:].rearrange("t j (q r) -> t j q r", r=RUN), k_sb[first + n].rearrange("t (q j r) -> t j q r", j=PACK, r=RUN),
                                         neg_mean[first][:, n:n + 1], rstd[first][:, n:n + 1], ALU.add, ALU.mult)
 
         def key_center_act(first, count):
@@ -139,7 +145,7 @@ def tile_lightningindexerheadweightedreluscore_x1_kernel(tc, c, wq, k, kg, kb, w
             nc.vector.scalar_tensor_tensor(neg_mean[first][:], mean_var[first][:, :, 0], -1.0, rstd[first][:], ALU.mult, ALU.mult)
             for n in range(count):
                 z[first + n] = work.tile([P, PACK, P], F32, name="z", bufs=4)
-                nc.scalar.activation(z[first + n][:], k_sb[first + n].rearrange("t (p j) -> t j p", j=PACK), ACT.Identity,
+                nc.scalar.activation(z[first + n][:].rearrange("t j (q r) -> t j q r", r=RUN), k_sb[first + n].rearrange("t (q j r) -> t j q r", j=PACK, r=RUN), ACT.Identity,
                                      bias=neg_mean[first][:, n:n + 1], scale=rstd[first][:, n:n + 1])
 
         key_bank = {}
@@ -151,11 +157,11 @@ def tile_lightningindexerheadweightedreluscore_x1_kernel(tc, c, wq, k, kg, kb, w
                 for n in range(4):
                     nc.tensor.transpose(bank[:, blk(n)], z[4 * th + n][:, j, :], ident[:])
                 nc.scalar.activation(kn_slots[th][:, j, :], bank[:], ACT.Identity,
-                                     bias=kb_col[:, j:j + 1], scale=kg_col[:, j:j + 1])
+                                     bias=gain_col[:, PACK + j:PACK + j + 1], scale=gain_col[:, j:j + 1])
 
         def key_pack(th, copy):
             kn_words[th] = work.tile([P, BANK, PACK], BF16, name="kn_words", bufs=1, align_bytes=64)
-            copy(kn_words[th][:], kn_slots[th][:].rearrange("p j t -> p t j"))
+            copy(kn_words[th][:].rearrange("p (c i) j -> p c j i", i=PACK), kn_slots[th][:].rearrange("p j (c i) -> p c j i", i=PACK))
 
         def key_quant(th):
             quantize(kn_mx, blk(th, BANK), kn_words[th][:].rearrange("p t j -> p (t j)"))
@@ -183,7 +189,14 @@ def tile_lightningindexerheadweightedreluscore_x1_kernel(tc, c, wq, k, kg, kb, w
 
         def wq_pack(h, first, count, copy, tag):
             wq_words[h, first] = work.tile([P, count, P, PACK], BF16, name=tag, bufs=1, align_bytes=64)
-            copy(wq_words[h, first][:], wq_sb[h][:].rearrange("p i (m j) -> p j m i", j=PACK)[:, first:first + count, :, :])
+            for j in range(first, first + count):
+                dst = wq_words[h, first][:, j - first, :, :]
+                if copy is pool_copy:
+                    src = wq_sb[h][:].rearrange("p i (q j r) -> p j q r i", j=PACK, r=RUN)
+                    copy(dst.rearrange("p (q r) i -> p q r i", r=RUN), src[:, j, :, :, :])
+                else:
+                    src = wq_sb[h][:].rearrange("p i (q j u r) -> p j q u i r", j=PACK, u=2, r=4)
+                    copy(dst.rearrange("p (q u r) i -> p q u i r", u=2, r=4), src[:, j, :, :, :, :])
 
         def wq_quant(h, first, count):
             if h not in wq_mx:
@@ -260,8 +273,8 @@ def tile_lightningindexerheadweightedreluscore_x1_kernel(tc, c, wq, k, kg, kb, w
 
         def f_second(su, j, cols=slice(0, BANK)):
             g, th = divmod(su, 2)
-            if j == 0:
-                res[su] = work.tile([P, PACK, BANK], F32, name="res")
+            if su not in res:
+                res[su] = work.tile([P, PACK, BANK], F32, name="res", tag="wq_then_res", bufs=4)
             nc.vector.scalar_tensor_tensor(res[su][:, j, cols], relu_d[su, j, 3][:, cols], weight(su, j, 3),
                                            part[su, j][:, cols], ALU.mult, ALU.add)
             rows = out_0[blk(g, BANK), blk(th, BANK)].rearrange("(p j) t -> p j t", j=PACK)
@@ -269,7 +282,11 @@ def tile_lightningindexerheadweightedreluscore_x1_kernel(tc, c, wq, k, kg, kb, w
 
         def res_pack(su, first, count, copy, tag):
             res_words[su, first] = work.tile([P, count * P, PACK], BF16, name=tag, bufs=2, align_bytes=64)
-            copy(res_words[su, first][:], res[su][:, :, first * P:(first + count) * P].rearrange("p j t -> p t j"))
+            src = res[su][:, :, first * P:(first + count) * P]
+            if copy is pool_copy:
+                copy(res_words[su, first][:], src.rearrange("p j t -> p t j"))
+            else:
+                copy(res_words[su, first][:].rearrange("p (c i) j -> p c j i", i=PACK), src.rearrange("p j (c i) -> p c j i", i=PACK))
 
         def res_quant(su, first, count):
             g, th = divmod(su, 2)
@@ -326,6 +343,7 @@ def tile_lightningindexerheadweightedreluscore_x1_kernel(tc, c, wq, k, kg, kb, w
         key_stats(2)
         key_stats(3)
         key_aggr(*g1)
+        gain_turn()
         key_rstd(*g1)
         key_center(*g0)
         c_in(0)
@@ -346,6 +364,8 @@ def tile_lightningindexerheadweightedreluscore_x1_kernel(tc, c, wq, k, kg, kb, w
         wq_pack(1, 2, 2, vec_copy, "act_words")
         weights(0, 0)
         c_in(1)
+        wq_pack(2, 3, 1, act_copy, "last_words2")
+        wq_pack(3, 3, 1, act_copy, "last_words3")
         key_quant(0)
         q_quant(0, 0)
         t_mms(0, 0, 0, 1, 2, 3)
@@ -360,7 +380,6 @@ def tile_lightningindexerheadweightedreluscore_x1_kernel(tc, c, wq, k, kg, kb, w
         c_quant(1)
         queries(1, 0)
         key_pack(1, vec_copy)
-        wq_pack(2, 3, 1, vec_copy, "act_words")
         q_quant(0, 1)
         t_mms(0, 1, 0, 1, 2, 3)
         key_quant(1)
@@ -373,45 +392,38 @@ def tile_lightningindexerheadweightedreluscore_x1_kernel(tc, c, wq, k, kg, kb, w
         t_mms(1, 0, 0, 1)
         t_outs(0, 1, 2, 3)
         t_mms(1, 0, 2, 3)
-        wq_pack(3, 3, 1, vec_copy, "act_words")
         wq_quant(3, 0, 3)
         q_quant(1, 0)
         wq_quant(3, 3, 1)
-        weights(1, 1)
-        q_mm(0, 3, 0)
-        q_out(0, 3, 0)
-        q_mm(0, 3, 1)
-        q_out(0, 3, 1)
+        queries(0, 3)
         t_outs(1, 0, 0, 1)
         t_mms(1, 1, 0, 1)
+        weights(1, 1)
         q_quant(0, 2)
         t_outs(1, 0, 2, 3)
-        q_quant(0, 3, 0, 2)
+        q_quant(0, 3)
 
         units = [(su, j) for su in range(4) for j in range(PACK)]
         todo_t = [(su, n, h) for su, h in ((1, 1), (2, 0), (2, 1), (3, 0), (3, 1)) for n in range(4)][2:]
-        todo_q = [(0, 3, 2), (0, 3, 3)] + [(1, 1, sj) for sj in range(PACK)] + [(1, h, sj) for sj in range(PACK) for h in (2, 3)]
+        todo_q = [(1, h, sj) for h in (1, 2, 3) for sj in range(PACK)]
 
         def unit_act(i):
             su, j = units[i]
-            for h in (2, 3):
-                d_mm(su, j, h)
-                d_out(su, j, h)
             for task in todo_q[2 * i:2 * i + 2]:
                 q_mm(*task)
                 q_out(*task)
+            for h in (2, 3):
+                d_mm(su, j, h)
+                d_out(su, j, h)
 
         def q_ready(i):
-            for g, h, sj in todo_q[2 * i:2 * i + 2]:
-                if h >= 2:
-                    q_quant(g, h, sj, 1)
-                elif sj == 3:
-                    q_quant(g, h)
+            if i in (0, 2, 4):
+                q_quant(1, i // 2 + 1)
 
-        t_count = [2, 2, 2, 0, 2, 2, 2, 2, 2, 1, 1, 0, 0, 0, 0, 0]
-        ahead = [1, 2, 3, 4, 5, 6, 7, 8, 9, 11, 13, 14, 15, 15, 15, 15]
-        f_turn(0, 0)
+        t_count = [2, 2, 2, 2, 2, 2, 2, 1, 1, 1, 1, 0, 0, 0, 0, 0]
+        ahead = [1, 2, 3, 4, 5, 6, 8, 10, 11, 12, 13, 14, 15, 15, 15, 15]
         issued = 1
+        f_turn(0, 0)
         unit_act(0)
         t_outs(1, 1, 0, 1)
         done = 0

@@ -71,6 +71,8 @@ def tile_lightningindexerheadweightedreluscore_x1_kernel(tc, c, wq, k, kg, kb, w
         load_wq(3)
 
         ident = keep.tile([P, P], F32, name="ident")
+        ident_bf = keep.tile([P, P], BF16, name="ident_bf")
+        make_identity(nc, ident_bf[:])
         make_identity(nc, ident[:])
         w_col = keep.tile([P, 2, PACK * H], F32, name="w_col")
         gain_wide = keep.tile([P, P], F32, name="gain_wide")
@@ -82,7 +84,7 @@ def tile_lightningindexerheadweightedreluscore_x1_kernel(tc, c, wq, k, kg, kb, w
             nc.gpsimd.tensor_scalar(gain_wide[0:2 * PACK, :], gain_rows[:], 1.0, 1.0, ALU.mult, ALU.mult)
 
         def gain_turn():
-            bank = bank_v()
+            bank = bank_a()
             nc.tensor.transpose(bank[:, 0:P], gain_wide[:], ident[:])
             nc.scalar.copy(out=gain_col[:], in_=bank[:, 0:2 * PACK])
 
@@ -117,9 +119,9 @@ def tile_lightningindexerheadweightedreluscore_x1_kernel(tc, c, wq, k, kg, kb, w
             stats[tt] = keep.tile([P, 6], F32, name="stats%d" % tt)
             nc.vector.bn_stats(stats[tt][:], k_sb[tt])
 
-        def key_aggr(first, count):
+        def key_aggr(first, count, order):
             mean_var[first] = keep.tile([P, count, 2], F32, name="mean_var%d" % first)
-            for n in range(count):
+            for n in order:
                 nc.vector.bn_aggr(mean_var[first][:, n, :], stats[first + n][:])
 
         def key_rstd(first, count):
@@ -224,15 +226,15 @@ def tile_lightningindexerheadweightedreluscore_x1_kernel(tc, c, wq, k, kg, kb, w
         w_row, w_bank = {}, {}
 
         def w_turn(g, h):
-            bank = bank_a()
+            bank = bank_v()
             w_bank[g, h] = bank
             for j in range(PACK):
-                col = w_col[:, g, j * H + h:j * H + h + 1]
-                nc.tensor.transpose(bank[:, blk(j)], col.to_broadcast([P, P]), ident[:])
+                col = w_sb[:, g, j * H + h:j * H + h + 1]
+                nc.tensor.matmul(bank[:, blk(j)], lhsT=col.to_broadcast([P, P]), rhs=ident_bf[:], start=True, stop=True)
 
         def w_out(g, h):
             w_row[g, h] = keep.tile([P, BANK], F32, name="w_row%d%d" % (g, h))
-            nc.scalar.copy(out=w_row[g, h][:], in_=w_bank[g, h][:])
+            nc.scalar.activation(w_row[g, h][:], w_bank[g, h][:], ACT.Copy, scale=1.0 / math.sqrt(D))
 
         t_bank, r_t, d_bank, relu_d, f_bank, part, res, res_words = {}, {}, {}, {}, {}, {}, {}, {}
         res_codes, res_scales = {}, {}
@@ -243,7 +245,7 @@ def tile_lightningindexerheadweightedreluscore_x1_kernel(tc, c, wq, k, kg, kb, w
             mx(t_bank[su, n, h][:], kn_mx, blk(4 * th + n), q_mx[g, h], slice(0, BANK))
 
         def t_out(su, n, h):
-            r_t[su, n, h] = work.tile([P, BANK], F32, name="r_t", bufs=20)
+            r_t[su, n, h] = work.tile([P, BANK], F32, name="r_t", bufs=24)
             nc.vector.scalar_tensor_tensor(r_t[su, n, h][:], t_bank[su, n, h][:], 0.0, w_row[su // 2, h][:], ALU.max, ALU.mult)
 
         def d_mm(su, j, h):
@@ -299,20 +301,26 @@ def tile_lightningindexerheadweightedreluscore_x1_kernel(tc, c, wq, k, kg, kb, w
                                   scales=res_scales[g][:, th * BANK + cols.start:th * BANK + cols.stop],
                                   in_=res_words[su, first][:].rearrange("p t j -> p (t j)"))
 
-        def res_store(su):
+        def res_store(su, cols=slice(0, BANK)):
             g, th = divmod(su, 2)
-            dst = out_1[g].rearrange("p m t -> p (m t)").bitcast(I32)
-            nc.sync.dma_start(out=dst[:, blk(th, BANK)], in_=res_codes[su][:].bitcast(I32))
-            if th == 1:
-                for q in range(4):
-                    eng = nc.scalar if (g == 1 and q % 2 == 1) else nc.sync
-                    eng.dma_start(out=out_2[g, 4 * q:4 * q + 4, :].bitcast(I32),
-                                  in_=res_scales[g][32 * q:32 * q + 4, :].bitcast(I32))
+            dst = out_1[g].rearrange("p m t -> p (m t)").bitcast(I32)[:, blk(th, BANK)]
+            nc.sync.dma_start(out=dst[:, cols], in_=res_codes[su][:, cols].bitcast(I32))
+
+        def scale_store(g):
+            for q in range(4):
+                eng = nc.scalar if (g == 1 and q % 2 == 1) else nc.sync
+                eng.dma_start(out=out_2[g, 4 * q:4 * q + 4, :].bitcast(I32),
+                              in_=res_scales[g][32 * q:32 * q + 4, :].bitcast(I32))
 
         g0, g1, g2 = key_groups
 
         def queries(g, h):
             for sj in range(PACK):
+                q_mm(g, h, sj)
+                q_out(g, h, sj)
+
+        def query_half(g, h, first):
+            for sj in (first, first + 1):
                 q_mm(g, h, sj)
                 q_out(g, h, sj)
 
@@ -336,17 +344,22 @@ def tile_lightningindexerheadweightedreluscore_x1_kernel(tc, c, wq, k, kg, kb, w
         key_stats(0)
         key_stats(1)
         constants()
-        key_aggr(*g0)
+        key_aggr(*g0, (0, 1))
         key_rstd(*g0)
+        for g in range(2):
+            for h in range(2):
+                w_turn(g, h)
         wq_pack(0, 0, 2, pool_copy, "pool_words")
         wq_pack(0, 2, 2, act_copy, "act_words")
         key_stats(2)
         key_stats(3)
-        key_aggr(*g1)
+        key_aggr(*g1, (0, 1))
         gain_turn()
+        w_out(0, 0)
         key_rstd(*g1)
         key_center(*g0)
         c_in(0)
+        w_out(0, 1)
         wq_quant(0, 2, 2)
         key_center(*g1)
         key_stats(4)
@@ -358,53 +371,61 @@ def tile_lightningindexerheadweightedreluscore_x1_kernel(tc, c, wq, k, kg, kb, w
         key_stats(5)
         key_stats(6)
         key_stats(7)
-        key_aggr(*g2)
+        key_aggr(*g2, (2, 0, 1, 3))
         key_rstd(*g2)
         key_pack(0, vec_copy)
         wq_pack(1, 2, 2, vec_copy, "act_words")
-        weights(0, 0)
+        w_out(1, 0)
+        w_out(1, 1)
         c_in(1)
-        wq_pack(2, 3, 1, act_copy, "last_words2")
-        wq_pack(3, 3, 1, act_copy, "last_words3")
+        wq_pack(2, 2, 2, act_copy, "last_words2")
         key_quant(0)
         q_quant(0, 0)
         t_mms(0, 0, 0, 1, 2, 3)
         key_center(*g2)
         keys_out(1)
         wq_quant(1, 2, 2)
-        wq_quant(1, 0, 2)
-        wq_pack(2, 0, 3, pool_copy, "pool_words")
-        queries(0, 1)
-        weights(0, 1)
-        t_outs(0, 0, 0, 1, 2, 3)
         c_quant(1)
+        wq_quant(1, 0, 2)
+        wq_pack(2, 0, 2, pool_copy, "pool_words")
+        queries(0, 1)
+        wq_pack(3, 3, 1, act_copy, "last_words3")
+        t_outs(0, 0, 3, 2, 1, 0)
         queries(1, 0)
         key_pack(1, vec_copy)
+        wq_quant(2, 2, 2)
+        key_quant(1)
         q_quant(0, 1)
         t_mms(0, 1, 0, 1, 2, 3)
-        key_quant(1)
-        wq_quant(2, 3, 1)
-        wq_quant(2, 0, 3)
+        wq_quant(3, 3, 1)
+        wq_quant(2, 0, 2)
         wq_pack(3, 0, 3, pool_copy, "pool_words")
-        weights(1, 0)
-        queries(0, 2)
+        query_half(0, 2, 0)
         t_outs(0, 1, 0, 1)
         t_mms(1, 0, 0, 1)
-        t_outs(0, 1, 2, 3)
+        query_half(0, 2, 2)
+        t_outs(0, 1, 3, 2)
         t_mms(1, 0, 2, 3)
+        t_outs(1, 0, 1)
         wq_quant(3, 0, 3)
-        q_quant(1, 0)
-        wq_quant(3, 3, 1)
         queries(0, 3)
-        t_outs(1, 0, 0, 1)
+        q_quant(1, 0)
+        t_outs(1, 0, 0)
         t_mms(1, 1, 0, 1)
-        weights(1, 1)
         q_quant(0, 2)
-        t_outs(1, 0, 2, 3)
+        t_outs(1, 0, 3, 2)
+        d_mm(0, 0, 2)
+        d_out(0, 0, 2)
+        t_mms(1, 1, 2, 3)
+        query_half(1, 1, 0)
+        t_outs(1, 1, 0)
+        f_turn(0, 0)
         q_quant(0, 3)
+        d_mm(0, 0, 3)
+        d_out(0, 0, 3)
 
         units = [(su, j) for su in range(4) for j in range(PACK)]
-        todo_t = [(su, n, h) for su, h in ((1, 1), (2, 0), (2, 1), (3, 0), (3, 1)) for n in range(4)][2:]
+        todo_t = [(su, n, h) for su, h in ((1, 1), (2, 0), (2, 1), (3, 0), (3, 1)) for n in range(4)][4:]
         todo_q = [(1, h, sj) for h in (1, 2, 3) for sj in range(PACK)]
 
         def unit_act(i):
@@ -412,20 +433,15 @@ def tile_lightningindexerheadweightedreluscore_x1_kernel(tc, c, wq, k, kg, kb, w
             for task in todo_q[2 * i:2 * i + 2]:
                 q_mm(*task)
                 q_out(*task)
-            for h in (2, 3):
-                d_mm(su, j, h)
-                d_out(su, j, h)
+            d_mm(su, j, 3)
+            d_mm(su, j, 2)
+            d_out(su, j, 2)
+            d_out(su, j, 3)
 
-        def q_ready(i):
-            if i in (0, 2, 4):
-                q_quant(1, i // 2 + 1)
-
-        t_count = [2, 2, 2, 2, 2, 2, 2, 1, 1, 1, 1, 0, 0, 0, 0, 0]
+        t_count = [2, 1, 2, 2, 2, 2, 1, 1, 1, 1, 1, 0, 0, 0, 0, 0]
         ahead = [1, 2, 3, 4, 5, 6, 8, 10, 11, 12, 13, 14, 15, 15, 15, 15]
+        t_outs(1, 1, 1, 3, 2)
         issued = 1
-        f_turn(0, 0)
-        unit_act(0)
-        t_outs(1, 1, 0, 1)
         done = 0
         for i, (su, j) in enumerate(units[:-1]):
             mine = todo_t[done:done + t_count[i]]
@@ -435,15 +451,14 @@ def tile_lightningindexerheadweightedreluscore_x1_kernel(tc, c, wq, k, kg, kb, w
             while issued < min(16, ahead[i] + 1):
                 unit_act(issued)
                 issued = issued + 1
-            if mine:
-                t_out(*mine[0])
             f_first(su, j)
-            if len(mine) > 1:
-                t_out(*mine[1])
+            for t in reversed(mine):
+                t_out(*t)
             f_turn(*units[i + 1])
             if i > 0:
                 f_second(*units[i - 1])
-            q_ready(i)
+            if i in (1, 3, 5):
+                q_quant(1, i // 2 + 1)
             if i in (7, 8, 9, 10):
                 res_quant(0, i - 7, 1)
             if i == 10:
@@ -456,17 +471,20 @@ def tile_lightningindexerheadweightedreluscore_x1_kernel(tc, c, wq, k, kg, kb, w
                 res_quant(1, 2 * (i - 11), 2)
             if i == 12:
                 res_store(1)
+                scale_store(0)
         halves = (slice(0, 256), slice(256, 512))
         f_first(3, 3, halves[0])
-        f_second(3, 2)
         f_first(3, 3, halves[1])
-        res_quant(2, 0, 2)
+        f_second(3, 2)
         f_second(3, 3, halves[0])
-        res_pack(3, 0, 2, act_copy, "act_res")
+        res_pack(3, 0, 2, act_copy, "tail_a")
+        f_second(3, 3, halves[1])
+        res_quant(2, 0, 2)
+        res_pack(3, 2, 2, vec_copy, "tail_b")
         res_quant(2, 2, 2)
         res_store(2)
-        f_second(3, 3, halves[1])
-        res_pack(3, 2, 2, vec_copy, "pool_res")
-        res_quant(3, 0, 2)
         res_quant(3, 2, 2)
-        res_store(3)
+        res_store(3, halves[1])
+        res_quant(3, 0, 2)
+        res_store(3, halves[0])
+        scale_store(1)

@@ -17,10 +17,19 @@ ALU = mybir.AluOpType
 ACT = mybir.ActivationFunctionType
 
 P = 128
-PACK = 4
+SLOTS = 4
 BANK = 512
-EPS = 1e-6
 RUN = 8
+EPS = 1e-6
+SCORE_SCALE = 1.0 / math.sqrt(D)
+UNITS = [(quarter, slot) for quarter in range(4) for slot in range(SLOTS)]
+QUERY_UNITS = 6
+DOUBLE_STEPS = 6
+MAX_LEAD = 3
+
+
+def blk(n, width=P):
+    return slice(n * width, (n + 1) * width)
 
 
 def tile_lightningindexerheadweightedreluscore_x1_kernel(tc, c, wq, k, kg, kb, w, out_0, out_1, out_2):
@@ -28,43 +37,43 @@ def tile_lightningindexerheadweightedreluscore_x1_kernel(tc, c, wq, k, kg, kb, w
     with ExitStack() as ctx:
         keep = ctx.enter_context(tc.tile_pool(name="keep", bufs=1))
         work = ctx.enter_context(tc.tile_pool(name="work", bufs=2))
-        psum = ctx.enter_context(tc.psum_pool(name="psum", bufs=2))
+        psum = ctx.enter_context(tc.psum_pool(name="psum", bufs=4))
         ctx.enter_context(tc.manual_schedule())
 
-        def bank_a():
-            return psum.tile([P, BANK], F32, name="bank_a", bufs=4)
+        def scalar_bank():
+            return psum.tile([P, BANK], F32, name="scalar_bank")
 
-        def bank_v():
-            return psum.tile([P, BANK], F32, name="bank_v", bufs=4)
+        def vector_bank():
+            return psum.tile([P, BANK], F32, name="vector_bank")
 
-        key_groups = [(0, 2), (2, 2), (4, 4)]
+        keys_a, keys_b, keys_c = (0, 2), (2, 2), (4, 4)
         k_sb, c_sb, wq_sb = {}, {}, {}
 
         def load_k(first, count):
-            t = keep.tile([P, count, D], BF16, name="k_sb%d" % first)
-            nc.sync.dma_start(out=t[:], in_=k[first * P:(first + count) * P, :].rearrange("(n p) d -> p n d", p=P))
+            rows = keep.tile([P, count, D], BF16, name="k_sb%d" % first)
+            nc.sync.dma_start(out=rows[:], in_=k[first * P:(first + count) * P, :].rearrange("(n p) d -> p n d", p=P))
             for n in range(count):
-                k_sb[first + n] = t[:, n, :]
+                k_sb[first + n] = rows[:, n, :]
 
         def load_c(g):
-            c_sb[g] = keep.tile([P, PACK, C], BF16, name="c_sb%d" % g)
-            nc.sync.dma_start(out=c_sb[g][:], in_=c[g * BANK:(g + 1) * BANK, :].rearrange("(p j) i -> p j i", j=PACK))
+            c_sb[g] = keep.tile([P, SLOTS, C], BF16, name="c_sb%d" % g)
+            nc.sync.dma_start(out=c_sb[g][:], in_=c[blk(g, BANK), :].rearrange("(p j) i -> p j i", j=SLOTS))
 
         def load_wq(h):
-            wq_sb[h] = work.tile([P, PACK, D], BF16, name="wq_sb%d" % h, tag="wq_then_res", bufs=4)
-            nc.sync.dma_start(out=wq_sb[h][:], in_=wq[:, h, :].rearrange("(p i) d -> p i d", i=PACK))
+            wq_sb[h] = work.tile([P, SLOTS, D], BF16, name="wq_sb%d" % h, tag="wq_then_result", bufs=4)
+            nc.sync.dma_start(out=wq_sb[h][:], in_=wq[:, h, :].rearrange("(p i) d -> p i d", i=SLOTS))
 
-        w_sb = keep.tile([P, 2, PACK * H], BF16, name="w_sb")
-        gain_rows = keep.tile([2 * PACK, P], BF16, name="gain_rows")
-        load_k(*key_groups[0])
-        nc.scalar.dma_start(out=w_sb[:], in_=w.rearrange("(g p j) h -> p g (j h)", g=2, j=PACK))
-        for first, vec in ((0, kg), (PACK, kb)):
-            nc.scalar.dma_start(out=gain_rows[first:first + PACK, :].rearrange("j (q r) -> j q r", r=RUN),
-                                in_=vec.rearrange("(q j r) -> j q r", j=PACK, r=RUN))
+        w_sb = keep.tile([P, 2, SLOTS * H], BF16, name="w_sb")
+        gain_rows = keep.tile([2 * SLOTS, P], BF16, name="gain_rows")
+        load_k(*keys_a)
+        nc.scalar.dma_start(out=w_sb[:], in_=w.rearrange("(g p j) h -> p g (j h)", g=2, j=SLOTS))
+        for first, vec in ((0, kg), (SLOTS, kb)):
+            nc.scalar.dma_start(out=gain_rows[first:first + SLOTS, :].rearrange("j (b r) -> j b r", r=RUN),
+                                in_=vec.rearrange("(b j r) -> j b r", j=SLOTS, r=RUN))
+        load_k(*keys_b)
         load_wq(0)
-        load_k(*key_groups[1])
         load_c(0)
-        load_k(*key_groups[2])
+        load_k(*keys_c)
         load_wq(1)
         load_wq(2)
         load_c(1)
@@ -74,21 +83,21 @@ def tile_lightningindexerheadweightedreluscore_x1_kernel(tc, c, wq, k, kg, kb, w
         ident_bf = keep.tile([P, P], BF16, name="ident_bf")
         make_identity(nc, ident_bf[:])
         make_identity(nc, ident[:])
-        w_col = keep.tile([P, 2, PACK * H], F32, name="w_col")
+        w_col = keep.tile([P, 2, SLOTS * H], F32, name="w_col")
         gain_wide = keep.tile([P, P], F32, name="gain_wide")
-        gain_col = keep.tile([P, 2 * PACK], F32, name="gain_col")
+        gain_col = keep.tile([P, 2 * SLOTS], F32, name="gain_col")
         nc.gpsimd.memset(gain_wide[:], 0.0)
 
-        def constants():
-            nc.gpsimd.tensor_scalar(w_col[:], w_sb[:], 1.0 / math.sqrt(D), 1.0, ALU.mult, ALU.mult)
-            nc.gpsimd.tensor_scalar(gain_wide[0:2 * PACK, :], gain_rows[:], 1.0, 1.0, ALU.mult, ALU.mult)
+        def gpsimd_copy(out, in_):
+            nc.gpsimd.tensor_scalar(out, in_, 1.0, 1.0, ALU.mult, ALU.mult)
 
-        def gain_turn():
-            bank = bank_a()
-            nc.tensor.transpose(bank[:, 0:P], gain_wide[:], ident[:])
-            nc.scalar.copy(out=gain_col[:], in_=bank[:, 0:2 * PACK])
+        def vector_copy(out, in_):
+            nc.vector.tensor_copy(out=out, in_=in_)
 
-        def planes(name, width):
+        def scalar_copy(out, in_):
+            nc.scalar.copy(out=out, in_=in_)
+
+        def mx_tiles(name, width):
             codes = keep.tile([P, width], U32, name=name + "_codes", align_bytes=64)
             scales = keep.tile([P, width], U8, name=name + "_scales", align_bytes=64)
             return codes, scales
@@ -96,30 +105,29 @@ def tile_lightningindexerheadweightedreluscore_x1_kernel(tc, c, wq, k, kg, kb, w
         def quantize(dst, cols, src):
             nc.vector.quantize_mx(out=dst[0][:, cols].bitcast(FP8X4), scales=dst[1][:, cols], in_=src)
 
-        def mx(out, lhs, lcols, rhs, rcols):
-            nc.tensor.matmul_mx(out=out, lhsT=lhs[0][:, lcols].bitcast(FP8X4), lhsT_scale=lhs[1][:, lcols],
-                                rhs=rhs[0][:, rcols].bitcast(FP8X4), rhs_scale=rhs[1][:, rcols], start=True, stop=True)
+        def mx_matmul(out, lhs, lhs_cols, rhs, rhs_cols):
+            nc.tensor.matmul_mx(out=out, lhsT=lhs[0][:, lhs_cols].bitcast(FP8X4), lhsT_scale=lhs[1][:, lhs_cols],
+                                rhs=rhs[0][:, rhs_cols].bitcast(FP8X4), rhs_scale=rhs[1][:, rhs_cols],
+                                start=True, stop=True)
 
-        def blk(n, width=P):
-            return slice(n * width, (n + 1) * width)
+        def small_casts():
+            nc.gpsimd.tensor_scalar(w_col[:], w_sb[:], SCORE_SCALE, 1.0, ALU.mult, ALU.mult)
+            gpsimd_copy(gain_wide[0:2 * SLOTS, :], gain_rows[:])
 
-        def pool_copy(out, in_):
-            nc.gpsimd.tensor_scalar(out, in_, 1.0, 1.0, ALU.mult, ALU.mult)
+        def gains_to_partitions():
+            bank = scalar_bank()
+            nc.tensor.transpose(bank[:, 0:P], gain_wide[:], ident[:])
+            scalar_copy(gain_col[:], bank[:, 0:2 * SLOTS])
 
-        def vec_copy(out, in_):
-            nc.vector.tensor_copy(out=out, in_=in_)
+        kn_mx = mx_tiles("kn", T)
+        stats, mean_var, rstd, normed, kn_slots, kn_words = {}, {}, {}, {}, {}, {}
 
-        def act_copy(out, in_):
-            nc.scalar.copy(out=out, in_=in_)
+        def key_stats(*tiles):
+            for n in tiles:
+                stats[n] = keep.tile([P, 6], F32, name="stats%d" % n)
+                nc.vector.bn_stats(stats[n][:], k_sb[n])
 
-        kn_mx = planes("kn", T)
-        stats, mean_var, rstd, neg_mean, z, kn_slots, kn_words = {}, {}, {}, {}, {}, {}, {}
-
-        def key_stats(tt):
-            stats[tt] = keep.tile([P, 6], F32, name="stats%d" % tt)
-            nc.vector.bn_stats(stats[tt][:], k_sb[tt])
-
-        def key_aggr(first, count, order):
+        def key_moments(first, count, order):
             mean_var[first] = keep.tile([P, count, 2], F32, name="mean_var%d" % first)
             for n in order:
                 nc.vector.bn_aggr(mean_var[first][:, n, :], stats[first + n][:])
@@ -128,363 +136,315 @@ def tile_lightningindexerheadweightedreluscore_x1_kernel(tc, c, wq, k, kg, kb, w
             rstd[first] = keep.tile([P, count], F32, name="rstd%d" % first)
             nc.scalar.activation(rstd[first][:], mean_var[first][:, :, 1], ACT.Abs_reciprocal_sqrt, bias=EPS)
 
-        def key_center(first, count):
+        def key_normalize(first, count):
             for n in range(count):
-                z[first + n] = work.tile([P, PACK, P], F32, name="z", bufs=4)
-                nc.vector.tensor_scalar(z[first + n][:].rearrange("t j (q r) -> t j q r", r=RUN), k_sb[first + n].rearrange("t (q j r) -> t j q r", j=PACK, r=RUN),
+                normed[first + n] = work.tile([P, SLOTS, P], F32, name="normed", bufs=4)
+                nc.vector.tensor_scalar(normed[first + n][:].rearrange("t j (b r) -> t j b r", r=RUN),
+                                        k_sb[first + n].rearrange("t (b j r) -> t j b r", j=SLOTS, r=RUN),
                                         mean_var[first][:, n, 0:1], rstd[first][:, n:n + 1], ALU.subtract, ALU.mult)
 
-        def key_center_pool(first, count):
-            neg_mean[first] = keep.tile([P, count], F32, name="neg_mean%d" % first)
-            nc.gpsimd.tensor_scalar(neg_mean[first][:], mean_var[first][:, :, 0], -1.0, 1.0, ALU.mult, ALU.mult)
-            for n in range(count):
-                z[first + n] = work.tile([P, PACK, P], F32, name="z", bufs=4)
-                nc.gpsimd.tensor_scalar(z[first + n][:].rearrange("t j (q r) -> t j q r", r=RUN), k_sb[first + n].rearrange("t (q j r) -> t j q r", j=PACK, r=RUN),
-                                        neg_mean[first][:, n:n + 1], rstd[first][:, n:n + 1], ALU.add, ALU.mult)
-
-        def key_center_act(first, count):
-            neg_mean[first] = keep.tile([P, count], F32, name="neg_mean%d" % first)
-            nc.vector.scalar_tensor_tensor(neg_mean[first][:], mean_var[first][:, :, 0], -1.0, rstd[first][:], ALU.mult, ALU.mult)
-            for n in range(count):
-                z[first + n] = work.tile([P, PACK, P], F32, name="z", bufs=4)
-                nc.scalar.activation(z[first + n][:].rearrange("t j (q r) -> t j q r", r=RUN), k_sb[first + n].rearrange("t (q j r) -> t j q r", j=PACK, r=RUN), ACT.Identity,
-                                     bias=neg_mean[first][:, n:n + 1], scale=rstd[first][:, n:n + 1])
-
-        key_bank = {}
-
-        def keys_out(th):
-            kn_slots[th] = work.tile([P, PACK, BANK], BF16, name="kn_slots", bufs=1)
-            for j in range(PACK):
-                bank = bank_a()
+        def key_turn(half):
+            kn_slots[half] = work.tile([P, SLOTS, BANK], BF16, name="kn_slots", bufs=1)
+            for j in range(SLOTS):
+                bank = scalar_bank()
                 for n in range(4):
-                    nc.tensor.transpose(bank[:, blk(n)], z[4 * th + n][:, j, :], ident[:])
-                nc.scalar.activation(kn_slots[th][:, j, :], bank[:], ACT.Identity,
-                                     bias=gain_col[:, PACK + j:PACK + j + 1], scale=gain_col[:, j:j + 1])
+                    nc.tensor.transpose(bank[:, blk(n)], normed[4 * half + n][:, j, :], ident[:])
+                nc.scalar.activation(kn_slots[half][:, j, :], bank[:], ACT.Identity,
+                                     bias=gain_col[:, SLOTS + j:SLOTS + j + 1], scale=gain_col[:, j:j + 1])
 
-        def key_pack(th, copy):
-            kn_words[th] = work.tile([P, BANK, PACK], BF16, name="kn_words", bufs=1, align_bytes=64)
-            copy(kn_words[th][:].rearrange("p (c i) j -> p c j i", i=PACK), kn_slots[th][:].rearrange("p j (c i) -> p c j i", i=PACK))
+        def key_pack(half):
+            kn_words[half] = work.tile([P, BANK, SLOTS], BF16, name="kn_words", bufs=1, align_bytes=64)
+            vector_copy(kn_words[half][:].rearrange("p (m e) j -> p m j e", e=4),
+                        kn_slots[half][:].rearrange("p j (m e) -> p m j e", e=4))
 
-        def key_quant(th):
-            quantize(kn_mx, blk(th, BANK), kn_words[th][:].rearrange("p t j -> p (t j)"))
+        def key_quantize(half):
+            quantize(kn_mx, blk(half, BANK), kn_words[half][:].rearrange("p t j -> p (t j)"))
 
-        c_mx, c_words, c_bank, wq_mx, wq_words = {}, {}, {}, {}, {}
+        c_mx, c_words, wq_mx, wq_words = {}, {}, {}, {}
 
-        def c_turn(g, b):
+        def c_turn(g):
             words = c_sb[g][:].rearrange("p j i -> p (j i)").bitcast(F32)
-            bank = bank_a()
-            c_bank[g, b] = bank
-            for jj in range(2):
-                j = 2 * b + jj
-                for u in range(2):
-                    nc.tensor.transpose(bank[:, blk(2 * jj + u)], words[:, j * 256 + u:(j + 1) * 256:2], ident[:])
+            c_words[g] = work.tile([P, BANK * SLOTS], BF16, name="c_words", bufs=1, align_bytes=64)
+            for pair in range(2):
+                bank = scalar_bank()
+                for jj in range(2):
+                    j = 2 * pair + jj
+                    for u in range(2):
+                        nc.tensor.transpose(bank[:, blk(2 * jj + u)], words[:, j * 256 + u:(j + 1) * 256:2], ident[:])
+                scalar_copy(c_words[g][:, blk(pair, 1024)].bitcast(F32).rearrange("p (jj r u) -> p jj r u", jj=2, u=2),
+                            bank[:].rearrange("p (jj u r) -> p jj r u", jj=2, u=2))
 
-        def c_out(g, b):
-            if b == 0:
-                c_words[g] = work.tile([P, BANK * PACK], BF16, name="c_words", bufs=1, align_bytes=64)
-            dst = c_words[g][:, blk(b, 1024)].bitcast(F32).rearrange("p (jj r u) -> p jj r u", jj=2, u=2)
-            nc.scalar.copy(out=dst, in_=c_bank[g, b][:].rearrange("p (jj u r) -> p jj r u", jj=2, u=2))
-
-        def c_quant(g):
-            c_mx[g] = planes("c%d" % g, BANK)
+        def c_quantize(g):
+            c_mx[g] = mx_tiles("c%d" % g, BANK)
             quantize(c_mx[g], slice(0, BANK), c_words[g][:])
 
-        def wq_pack(h, first, count, copy, tag):
-            wq_words[h, first] = work.tile([P, count, P, PACK], BF16, name=tag, bufs=1, align_bytes=64)
+        def wq_pack(h, first, count, copy, stage):
+            wq_words[h, first] = work.tile([P, count, P, SLOTS], BF16, name=stage, bufs=1, align_bytes=64)
             for j in range(first, first + count):
                 dst = wq_words[h, first][:, j - first, :, :]
-                if copy is pool_copy:
-                    src = wq_sb[h][:].rearrange("p i (q j r) -> p j q r i", j=PACK, r=RUN)
-                    copy(dst.rearrange("p (q r) i -> p q r i", r=RUN), src[:, j, :, :, :])
+                if copy is gpsimd_copy:
+                    src = wq_sb[h][:].rearrange("p i (b j r) -> p j b r i", j=SLOTS, r=RUN)
+                    copy(dst.rearrange("p (b r) i -> p b r i", r=RUN), src[:, j, :, :, :])
                 else:
-                    src = wq_sb[h][:].rearrange("p i (q j u r) -> p j q u i r", j=PACK, u=2, r=4)
-                    copy(dst.rearrange("p (q u r) i -> p q u i r", u=2, r=4), src[:, j, :, :, :, :])
+                    src = wq_sb[h][:].rearrange("p i (b j u e) -> p j b u i e", j=SLOTS, u=2, e=4)
+                    copy(dst.rearrange("p (b u e) i -> p b u i e", u=2, e=4), src[:, j, :, :, :, :])
 
-        def wq_quant(h, first, count):
+        def wq_quantize(h, first, count):
             if h not in wq_mx:
-                wq_mx[h] = planes("wq%d" % h, D)
-            quantize(wq_mx[h], slice(first * P, (first + count) * P), wq_words[h, first][:].rearrange("p j m i -> p (j m i)"))
+                wq_mx[h] = mx_tiles("wq%d" % h, D)
+            quantize(wq_mx[h], slice(first * P, (first + count) * P),
+                     wq_words[h, first][:].rearrange("p j m i -> p (j m i)"))
 
-        q_mx, q_words, q_bank = {}, {}, {}
+        q_mx, q_words = {}, {}
 
-        def q_mm(g, h, sj):
-            bank = bank_a()
-            q_bank[g, h, sj] = bank
-            for j in range(PACK):
-                mx(bank[:, blk(j)], wq_mx[h], blk(j), c_mx[g], blk(sj))
+        def queries(g, h, slots=range(SLOTS)):
+            for slot in slots:
+                bank = scalar_bank()
+                for j in range(SLOTS):
+                    mx_matmul(bank[:, blk(j)], wq_mx[h], blk(j), c_mx[g], blk(slot))
+                if slot == 0:
+                    q_words[g, h] = work.tile([P, BANK, SLOTS], BF16, name="q_words", bufs=3, align_bytes=64)
+                    q_mx[g, h] = mx_tiles("q%d%d" % (g, h), BANK)
+                scalar_copy(q_words[g, h][:, blk(slot), :], bank[:].rearrange("p (j n) -> p n j", j=SLOTS))
 
-        def q_out(g, h, sj, copy=act_copy):
-            if sj == 0:
-                q_words[g, h] = work.tile([P, BANK, PACK], BF16, name="q_words", bufs=3, align_bytes=64)
-                q_mx[g, h] = planes("q%d%d" % (g, h), BANK)
-            copy(q_words[g, h][:, blk(sj), :], q_bank[g, h, sj][:].rearrange("p (j n) -> p n j", j=PACK))
-
-        def q_quant(g, h, first=0, count=PACK):
-            cols = slice(first * P, (first + count) * P)
-            quantize(q_mx[g, h], cols, q_words[g, h][:, cols, :].rearrange("p s j -> p (s j)"))
+        def query_quantize(g, h):
+            quantize(q_mx[g, h], slice(0, BANK), q_words[g, h][:].rearrange("p s j -> p (s j)"))
 
         w_row, w_bank = {}, {}
 
-        def w_turn(g, h):
-            bank = bank_v()
-            w_bank[g, h] = bank
-            for j in range(PACK):
+        def weight_spread(g, h):
+            w_bank[g, h] = vector_bank()
+            for j in range(SLOTS):
                 col = w_sb[:, g, j * H + h:j * H + h + 1]
-                nc.tensor.matmul(bank[:, blk(j)], lhsT=col.to_broadcast([P, P]), rhs=ident_bf[:], start=True, stop=True)
+                nc.tensor.matmul(w_bank[g, h][:, blk(j)], lhsT=col.to_broadcast([P, P]), rhs=ident_bf[:],
+                                 start=True, stop=True)
 
-        def w_out(g, h):
+        def weight_row(g, h):
             w_row[g, h] = keep.tile([P, BANK], F32, name="w_row%d%d" % (g, h))
-            nc.scalar.activation(w_row[g, h][:], w_bank[g, h][:], ACT.Copy, scale=1.0 / math.sqrt(D))
+            nc.scalar.activation(w_row[g, h][:], w_bank[g, h][:], ACT.Copy, scale=SCORE_SCALE)
 
-        t_bank, r_t, d_bank, relu_d, f_bank, part, res, res_words = {}, {}, {}, {}, {}, {}, {}, {}
-        res_codes, res_scales = {}, {}
+        km_bank, km_term, qm_bank, qm_relu, sum_bank, partial, result = {}, {}, {}, {}, {}, {}, {}
+        result_words, result_codes, result_scales = {}, {}, {}
 
-        def t_mm(su, n, h):
-            g, th = divmod(su, 2)
-            t_bank[su, n, h] = bank_v()
-            mx(t_bank[su, n, h][:], kn_mx, blk(4 * th + n), q_mx[g, h], slice(0, BANK))
+        def km_matmul(quarter, h, *tiles):
+            g, half = divmod(quarter, 2)
+            for n in tiles:
+                km_bank[quarter, h, n] = vector_bank()
+                mx_matmul(km_bank[quarter, h, n][:], kn_mx, blk(4 * half + n), q_mx[g, h], slice(0, BANK))
 
-        def t_out(su, n, h):
-            r_t[su, n, h] = work.tile([P, BANK], F32, name="r_t", bufs=24)
-            nc.vector.scalar_tensor_tensor(r_t[su, n, h][:], t_bank[su, n, h][:], 0.0, w_row[su // 2, h][:], ALU.max, ALU.mult)
+        def km_weigh(quarter, h, *tiles):
+            for n in tiles:
+                km_term[quarter, h, n] = work.tile([P, BANK], F32, name="km_term", bufs=24)
+                nc.vector.scalar_tensor_tensor(km_term[quarter, h, n][:], km_bank[quarter, h, n][:], 0.0,
+                                               w_row[quarter // 2, h][:], ALU.max, ALU.mult)
 
-        def d_mm(su, j, h):
-            g, th = divmod(su, 2)
-            d_bank[su, j, h] = bank_a()
-            mx(d_bank[su, j, h][:], q_mx[g, h], blk(j), kn_mx, blk(th, BANK))
+        def qm_matmul(quarter, slot, h):
+            g, half = divmod(quarter, 2)
+            qm_bank[quarter, slot, h] = scalar_bank()
+            mx_matmul(qm_bank[quarter, slot, h][:], q_mx[g, h], blk(slot), kn_mx, blk(half, BANK))
 
-        def d_out(su, j, h):
-            relu_d[su, j, h] = work.tile([P, BANK], F32, name="relu_d", bufs=10)
-            nc.scalar.activation(relu_d[su, j, h][:], d_bank[su, j, h][:], ACT.Relu)
+        def qm_clip(quarter, slot, h):
+            qm_relu[quarter, slot, h] = work.tile([P, BANK], F32, name="qm_relu", bufs=2 * (MAX_LEAD + 2))
+            nc.scalar.activation(qm_relu[quarter, slot, h][:], qm_bank[quarter, slot, h][:], ACT.Relu)
 
-        def f_turn(su, j):
-            f_bank[su, j] = bank_v()
+        def sum_turn(quarter, slot):
+            sum_bank[quarter, slot] = vector_bank()
             for n in range(4):
                 for h in range(2):
-                    nc.tensor.matmul(f_bank[su, j][:, blk(n)], lhsT=r_t[su, n, h][:, blk(j)], rhs=ident[:],
-                                     start=(h == 0), stop=(h == 1), is_transpose=True)
+                    nc.tensor.matmul(sum_bank[quarter, slot][:, blk(n)], lhsT=km_term[quarter, h, n][:, blk(slot)],
+                                     rhs=ident[:], start=(h == 0), stop=(h == 1), is_transpose=True)
 
-        def weight(su, j, h):
-            return w_col[:, su // 2, j * H + h:j * H + h + 1]
+        def weight(quarter, slot, h):
+            return w_col[:, quarter // 2, slot * H + h:slot * H + h + 1]
 
-        def f_first(su, j, cols=slice(0, BANK)):
-            if cols.start == 0:
-                part[su, j] = work.tile([P, BANK], F32, name="part", bufs=3)
-            nc.vector.scalar_tensor_tensor(part[su, j][:, cols], relu_d[su, j, 2][:, cols], weight(su, j, 2),
-                                           f_bank[su, j][:, cols], ALU.mult, ALU.add)
+        def add_head2(quarter, slot):
+            partial[quarter, slot] = work.tile([P, BANK], F32, name="partial", bufs=3)
+            nc.vector.scalar_tensor_tensor(partial[quarter, slot][:], qm_relu[quarter, slot, 2][:],
+                                           weight(quarter, slot, 2), sum_bank[quarter, slot][:], ALU.mult, ALU.add)
 
-        def f_second(su, j, cols=slice(0, BANK)):
-            g, th = divmod(su, 2)
-            if su not in res:
-                res[su] = work.tile([P, PACK, BANK], F32, name="res", tag="wq_then_res", bufs=4)
-            nc.vector.scalar_tensor_tensor(res[su][:, j, cols], relu_d[su, j, 3][:, cols], weight(su, j, 3),
-                                           part[su, j][:, cols], ALU.mult, ALU.add)
-            rows = out_0[blk(g, BANK), blk(th, BANK)].rearrange("(p j) t -> p j t", j=PACK)
-            nc.sync.dma_start(out=rows[:, j, cols], in_=res[su][:, j, cols])
+        def add_head3(quarter, slot, cols=slice(0, BANK)):
+            g, half = divmod(quarter, 2)
+            if slot == 0:
+                result[quarter] = work.tile([P, SLOTS, BANK], F32, name="result", tag="wq_then_result", bufs=4)
+            nc.vector.scalar_tensor_tensor(result[quarter][:, slot, cols], qm_relu[quarter, slot, 3][:, cols],
+                                           weight(quarter, slot, 3), partial[quarter, slot][:, cols], ALU.mult, ALU.add)
+            rows = out_0[blk(g, BANK), blk(half, BANK)].rearrange("(p j) t -> p j t", j=SLOTS)
+            nc.sync.dma_start(out=rows[:, slot, cols], in_=result[quarter][:, slot, cols])
 
-        def res_pack(su, first, count, copy, tag):
-            res_words[su, first] = work.tile([P, count * P, PACK], BF16, name=tag, bufs=2, align_bytes=64)
-            src = res[su][:, :, first * P:(first + count) * P]
-            if copy is pool_copy:
-                copy(res_words[su, first][:], src.rearrange("p j t -> p t j"))
+        def result_pack(quarter, first, count, copy, stage):
+            result_words[quarter, first] = work.tile([P, count * P, SLOTS], BF16, name=stage, align_bytes=64)
+            src = result[quarter][:, :, first * P:(first + count) * P]
+            if copy is gpsimd_copy:
+                copy(result_words[quarter, first][:], src.rearrange("p j t -> p t j"))
             else:
-                copy(res_words[su, first][:].rearrange("p (c i) j -> p c j i", i=PACK), src.rearrange("p j (c i) -> p c j i", i=PACK))
+                copy(result_words[quarter, first][:].rearrange("p (m e) j -> p m j e", e=4),
+                     src.rearrange("p j (m e) -> p m j e", e=4))
 
-        def res_quant(su, first, count):
-            g, th = divmod(su, 2)
-            if su not in res_codes:
-                res_codes[su] = work.tile([P, BANK], U32, name="res_codes", align_bytes=64)
-            if g not in res_scales:
-                res_scales[g] = keep.tile([P, T], U8, name="res_scales%d" % g, align_bytes=64)
+        def result_quantize(quarter, first, count):
+            g, half = divmod(quarter, 2)
+            if quarter not in result_codes:
+                result_codes[quarter] = work.tile([P, BANK], U32, name="result_codes", align_bytes=64)
+            if g not in result_scales:
+                result_scales[g] = keep.tile([P, T], U8, name="result_scales%d" % g, align_bytes=64)
             cols = slice(first * P, (first + count) * P)
-            nc.vector.quantize_mx(out=res_codes[su][:, cols].bitcast(FP8X4),
-                                  scales=res_scales[g][:, th * BANK + cols.start:th * BANK + cols.stop],
-                                  in_=res_words[su, first][:].rearrange("p t j -> p (t j)"))
+            nc.vector.quantize_mx(out=result_codes[quarter][:, cols].bitcast(FP8X4),
+                                  scales=result_scales[g][:, half * BANK + cols.start:half * BANK + cols.stop],
+                                  in_=result_words[quarter, first][:].rearrange("p t j -> p (t j)"))
 
-        def res_store(su, cols=slice(0, BANK)):
-            g, th = divmod(su, 2)
-            dst = out_1[g].rearrange("p m t -> p (m t)").bitcast(I32)[:, blk(th, BANK)]
-            nc.sync.dma_start(out=dst[:, cols], in_=res_codes[su][:, cols].bitcast(I32))
+        def store_codes(quarter, cols=slice(0, BANK)):
+            g, half = divmod(quarter, 2)
+            dst = out_1[g].rearrange("p m t -> p (m t)").bitcast(I32)[:, blk(half, BANK)]
+            nc.sync.dma_start(out=dst[:, cols], in_=result_codes[quarter][:, cols].bitcast(I32))
 
-        def scale_store(g):
+        def store_scales(g, queues):
             for q in range(4):
-                eng = nc.scalar if (g == 1 and q % 2 == 1) else nc.sync
-                eng.dma_start(out=out_2[g, 4 * q:4 * q + 4, :].bitcast(I32),
-                              in_=res_scales[g][32 * q:32 * q + 4, :].bitcast(I32))
+                queues[q % len(queues)].dma_start(out=out_2[g, 4 * q:4 * q + 4, :].bitcast(I32),
+                                                  in_=result_scales[g][32 * q:32 * q + 4, :].bitcast(I32))
 
-        g0, g1, g2 = key_groups
-
-        def queries(g, h):
-            for sj in range(PACK):
-                q_mm(g, h, sj)
-                q_out(g, h, sj)
-
-        def query_half(g, h, first):
-            for sj in (first, first + 1):
-                q_mm(g, h, sj)
-                q_out(g, h, sj)
-
-        def weights(g, h):
-            w_turn(g, h)
-            w_out(g, h)
-
-        def c_in(g):
-            for b in range(2):
-                c_turn(g, b)
-                c_out(g, b)
-
-        def t_mms(su, h, *ns):
-            for n in ns:
-                t_mm(su, n, h)
-
-        def t_outs(su, h, *ns):
-            for n in ns:
-                t_out(su, n, h)
-
-        key_stats(0)
-        key_stats(1)
-        constants()
-        key_aggr(*g0, (0, 1))
-        key_rstd(*g0)
+        key_stats(0, 1, 2)
+        small_casts()
+        key_moments(*keys_a, (1, 0))
+        key_rstd(*keys_a)
         for g in range(2):
             for h in range(2):
-                w_turn(g, h)
-        wq_pack(0, 0, 2, pool_copy, "pool_words")
-        wq_pack(0, 2, 2, act_copy, "act_words")
-        key_stats(2)
+                weight_spread(g, h)
+        wq_pack(0, 2, 2, scalar_copy, "engine_stage")
         key_stats(3)
-        key_aggr(*g1, (0, 1))
-        gain_turn()
-        w_out(0, 0)
-        key_rstd(*g1)
-        key_center(*g0)
-        c_in(0)
-        w_out(0, 1)
-        wq_quant(0, 2, 2)
-        key_center(*g1)
+        key_normalize(*keys_a)
+        key_moments(*keys_b, (1, 0))
+        key_rstd(*keys_b)
+        gains_to_partitions()
+        wq_pack(0, 0, 2, vector_copy, "gpsimd_stage")
+        weight_row(0, 0)
+        c_turn(0)
+        weight_row(0, 1)
+        key_normalize(*keys_b)
+        wq_quantize(0, 2, 2)
         key_stats(4)
-        c_quant(0)
-        wq_quant(0, 0, 2)
-        keys_out(0)
+        c_quantize(0)
+        wq_quantize(0, 0, 2)
+        key_turn(0)
         queries(0, 0)
-        wq_pack(1, 0, 2, pool_copy, "pool_words")
-        key_stats(5)
-        key_stats(6)
-        key_stats(7)
-        key_aggr(*g2, (2, 0, 1, 3))
-        key_rstd(*g2)
-        key_pack(0, vec_copy)
-        wq_pack(1, 2, 2, vec_copy, "act_words")
-        w_out(1, 0)
-        w_out(1, 1)
-        c_in(1)
-        wq_pack(2, 2, 2, act_copy, "last_words2")
-        key_quant(0)
-        q_quant(0, 0)
-        t_mms(0, 0, 0, 1, 2, 3)
-        key_center(*g2)
-        keys_out(1)
-        wq_quant(1, 2, 2)
-        c_quant(1)
-        wq_quant(1, 0, 2)
-        wq_pack(2, 0, 2, pool_copy, "pool_words")
+
+        wq_pack(1, 0, 2, gpsimd_copy, "gpsimd_stage")
+        key_stats(5, 6, 7)
+        key_moments(*keys_c, (2, 0, 1, 3))
+        key_rstd(*keys_c)
+        key_pack(0)
+        wq_pack(1, 2, 2, vector_copy, "engine_stage")
+        weight_row(1, 0)
+        weight_row(1, 1)
+        c_turn(1)
+        wq_pack(2, 2, 2, scalar_copy, "wq2_stage")
+        key_quantize(0)
+        query_quantize(0, 0)
+        km_matmul(0, 0, 0, 1, 2, 3)
+        key_normalize(*keys_c)
+        key_turn(1)
+        wq_quantize(1, 2, 2)
+        c_quantize(1)
+        wq_quantize(1, 0, 2)
+
+        wq_pack(2, 0, 2, gpsimd_copy, "gpsimd_stage")
         queries(0, 1)
-        wq_pack(3, 3, 1, act_copy, "last_words3")
-        t_outs(0, 0, 3, 2, 1, 0)
+        wq_pack(3, 3, 1, scalar_copy, "wq3_stage")
+        km_weigh(0, 0, 3, 2, 1, 0)
         queries(1, 0)
-        key_pack(1, vec_copy)
-        wq_quant(2, 2, 2)
-        key_quant(1)
-        q_quant(0, 1)
-        t_mms(0, 1, 0, 1, 2, 3)
-        wq_quant(3, 3, 1)
-        wq_quant(2, 0, 2)
-        wq_pack(3, 0, 3, pool_copy, "pool_words")
-        query_half(0, 2, 0)
-        t_outs(0, 1, 0, 1)
-        t_mms(1, 0, 0, 1)
-        query_half(0, 2, 2)
-        t_outs(0, 1, 3, 2)
-        t_mms(1, 0, 2, 3)
-        t_outs(1, 0, 1)
-        wq_quant(3, 0, 3)
+        key_pack(1)
+        wq_quantize(2, 2, 2)
+        key_quantize(1)
+        query_quantize(0, 1)
+        km_matmul(0, 1, 0, 1, 2, 3)
+        wq_quantize(3, 3, 1)
+        wq_quantize(2, 0, 2)
+        wq_pack(3, 0, 3, gpsimd_copy, "gpsimd_stage")
+        queries(0, 2, (0, 1))
+        km_weigh(0, 1, 0, 1)
+        km_matmul(1, 0, 0, 1)
+        queries(0, 2, (2, 3))
+        km_weigh(0, 1, 3, 2)
+        km_matmul(1, 0, 2, 3)
+        km_weigh(1, 0, 1)
+        wq_quantize(3, 0, 3)
         queries(0, 3)
-        q_quant(1, 0)
-        t_outs(1, 0, 0)
-        t_mms(1, 1, 0, 1)
-        q_quant(0, 2)
-        t_outs(1, 0, 3, 2)
-        d_mm(0, 0, 2)
-        d_out(0, 0, 2)
-        t_mms(1, 1, 2, 3)
-        query_half(1, 1, 0)
-        t_outs(1, 1, 0)
-        f_turn(0, 0)
-        q_quant(0, 3)
-        d_mm(0, 0, 3)
-        d_out(0, 0, 3)
+        query_quantize(1, 0)
+        km_weigh(1, 0, 0)
+        km_matmul(1, 1, 0, 1)
+        query_quantize(0, 2)
+        km_weigh(1, 0, 3, 2)
 
-        units = [(su, j) for su in range(4) for j in range(PACK)]
-        todo_t = [(su, n, h) for su, h in ((1, 1), (2, 0), (2, 1), (3, 0), (3, 1)) for n in range(4)][4:]
-        todo_q = [(1, h, sj) for h in (1, 2, 3) for sj in range(PACK)]
+        group1_queries = [(h, slot) for h in (1, 2, 3) for slot in range(SLOTS)]
+        group1_products = [(quarter, h, n) for h in range(2) for quarter in (2, 3) for n in range(4)]
 
-        def unit_act(i):
-            su, j = units[i]
-            for task in todo_q[2 * i:2 * i + 2]:
-                q_mm(*task)
-                q_out(*task)
-            d_mm(su, j, 3)
-            d_mm(su, j, 2)
-            d_out(su, j, 2)
-            d_out(su, j, 3)
+        def scalar_work(u):
+            quarter, slot = UNITS[u]
+            for h, query_slot in group1_queries[2 * u:2 * u + 2]:
+                queries(1, h, (query_slot,))
+            qm_matmul(quarter, slot, 3)
+            qm_matmul(quarter, slot, 2)
+            qm_clip(quarter, slot, 2)
+            qm_clip(quarter, slot, 3)
 
-        t_count = [2, 1, 2, 2, 2, 2, 1, 1, 1, 1, 1, 0, 0, 0, 0, 0]
-        ahead = [1, 2, 3, 4, 5, 6, 8, 10, 11, 12, 13, 14, 15, 15, 15, 15]
-        t_outs(1, 1, 1, 3, 2)
-        issued = 1
-        done = 0
-        for i, (su, j) in enumerate(units[:-1]):
-            mine = todo_t[done:done + t_count[i]]
-            done = done + t_count[i]
-            for t in mine:
-                t_mm(*t)
-            while issued < min(16, ahead[i] + 1):
-                unit_act(issued)
+        qm_matmul(0, 0, 2)
+        qm_clip(0, 0, 2)
+        queries(1, 1, (0, 1))
+        km_matmul(1, 1, 2, 3)
+        km_weigh(1, 1, 0)
+        sum_turn(0, 0)
+        query_quantize(0, 3)
+        qm_matmul(0, 0, 3)
+        qm_clip(0, 0, 3)
+        scalar_work(1)
+        km_weigh(1, 1, 1, 3, 2)
+
+        issued = 2
+        taken = 0
+        for step, (quarter, slot) in enumerate(UNITS[:-1]):
+            products = group1_products[taken:taken + (2 if step < DOUBLE_STEPS else 1)]
+            taken = taken + len(products)
+            for product in products:
+                km_matmul(*product)
+            lead = min(MAX_LEAD, max(1, step - QUERY_UNITS + 2))
+            while issued <= min(step + lead, len(UNITS) - 1):
+                scalar_work(issued)
                 issued = issued + 1
-            f_first(su, j)
-            for t in reversed(mine):
-                t_out(*t)
-            f_turn(*units[i + 1])
-            if i > 0:
-                f_second(*units[i - 1])
-            if i in (1, 3, 5):
-                q_quant(1, i // 2 + 1)
-            if i in (7, 8, 9, 10):
-                res_quant(0, i - 7, 1)
-            if i == 10:
-                res_store(0)
-            if i in (5, 6, 7, 8):
-                res_pack(0, i - 5, 1, pool_copy, "pool_res")
-            if i in (9, 10, 13, 14):
-                res_pack((i - 5) // 4, 2 * ((i - 5) % 4), 2, act_copy, "act_res")
-            if i in (11, 12):
-                res_quant(1, 2 * (i - 11), 2)
-            if i == 12:
-                res_store(1)
-                scale_store(0)
-        halves = (slice(0, 256), slice(256, 512))
-        f_first(3, 3, halves[0])
-        f_first(3, 3, halves[1])
-        f_second(3, 2)
-        f_second(3, 3, halves[0])
-        res_pack(3, 0, 2, act_copy, "tail_a")
-        f_second(3, 3, halves[1])
-        res_quant(2, 0, 2)
-        res_pack(3, 2, 2, vec_copy, "tail_b")
-        res_quant(2, 2, 2)
-        res_store(2)
-        res_quant(3, 2, 2)
-        res_store(3, halves[1])
-        res_quant(3, 0, 2)
-        res_store(3, halves[0])
-        scale_store(1)
+            for product in products[:1]:
+                km_weigh(*product)
+            add_head2(quarter, slot)
+            for product in products[1:]:
+                km_weigh(*product)
+            sum_turn(*UNITS[step + 1])
+            if step > 0:
+                add_head3(*UNITS[step - 1])
+            if step < QUERY_UNITS and step % 2 == 1:
+                query_quantize(1, step // 2 + 1)
+            late, part = divmod(step - 5, 4)
+            if 7 <= step <= 10:
+                result_quantize(0, step - 7, 1)
+            if step == 10:
+                store_codes(0)
+            if late == 0:
+                result_pack(0, part, 1, gpsimd_copy, "gpsimd_result")
+            if late > 0 and part < 2:
+                result_pack(late, 2 * part, 2, scalar_copy, "scalar_result")
+            if late == 1 and part >= 2:
+                result_quantize(1, 2 * (part - 2), 2)
+            if step == 12:
+                store_codes(1)
+                store_scales(0, [nc.sync])
+
+        low, high = slice(0, BANK // 2), slice(BANK // 2, BANK)
+        add_head2(3, 3)
+        add_head3(3, 2)
+        add_head3(3, 3, low)
+        result_pack(3, 0, 2, scalar_copy, "last_low")
+        add_head3(3, 3, high)
+        result_quantize(2, 0, 2)
+        result_pack(3, 2, 2, vector_copy, "last_high")
+        result_quantize(2, 2, 2)
+        store_codes(2)
+        result_quantize(3, 2, 2)
+        store_codes(3, high)
+        result_quantize(3, 0, 2)
+        store_codes(3, low)
+        store_scales(1, [nc.sync, nc.scalar])

from contextlib import ExitStack
import math

import concourse.mybir as mybir
from concourse.masks import make_identity

S, T, C, H, D = 1024, 1024, 512, 4, 512
FLOPS = 2 * S * C * H * D + 2 * H * S * T * D

F32 = mybir.dt.float32
BF16 = mybir.dt.bfloat16
U32 = mybir.dt.uint32
I32 = mybir.dt.int32
U8 = mybir.dt.uint8
FP8X4 = mybir.dt.float8_e4m3fn_x4
ALU = mybir.AluOpType
ACT = mybir.ActivationFunctionType

P = 128
SLOTS = 4
BANK = 512
RUN = 8
EPS = 1e-6
SCORE_SCALE = 1.0 / math.sqrt(D)
UNITS = [(quarter, slot) for quarter in range(4) for slot in range(SLOTS)]
QUERY_UNITS = 6
DOUBLE_STEPS = 6
MAX_LEAD = 3


def blk(n, width=P):
    return slice(n * width, (n + 1) * width)


def tile_lightningindexerheadweightedreluscore_x1_kernel(tc, c, wq, k, kg, kb, w, out_0, out_1, out_2):
    nc = tc.nc
    with ExitStack() as ctx:
        keep = ctx.enter_context(tc.tile_pool(name="keep", bufs=1))
        work = ctx.enter_context(tc.tile_pool(name="work", bufs=2))
        psum = ctx.enter_context(tc.psum_pool(name="psum", bufs=4))
        ctx.enter_context(tc.manual_schedule())

        def scalar_bank():
            return psum.tile([P, BANK], F32, name="scalar_bank")

        def vector_bank():
            return psum.tile([P, BANK], F32, name="vector_bank")

        keys_a, keys_b, keys_c = (0, 2), (2, 2), (4, 4)
        k_sb, c_sb, wq_sb = {}, {}, {}

        def load_k(first, count):
            rows = keep.tile([P, count, D], BF16, name="k_sb%d" % first)
            nc.sync.dma_start(out=rows[:], in_=k[first * P:(first + count) * P, :].rearrange("(n p) d -> p n d", p=P))
            for n in range(count):
                k_sb[first + n] = rows[:, n, :]

        def load_c(g):
            c_sb[g] = keep.tile([P, SLOTS, C], BF16, name="c_sb%d" % g)
            nc.sync.dma_start(out=c_sb[g][:], in_=c[blk(g, BANK), :].rearrange("(p j) i -> p j i", j=SLOTS))

        def load_wq(h):
            wq_sb[h] = work.tile([P, SLOTS, D], BF16, name="wq_sb%d" % h, tag="wq_then_result", bufs=4)
            nc.sync.dma_start(out=wq_sb[h][:], in_=wq[:, h, :].rearrange("(p i) d -> p i d", i=SLOTS))

        w_sb = keep.tile([P, 2, SLOTS * H], BF16, name="w_sb")
        gain_rows = keep.tile([2 * SLOTS, P], BF16, name="gain_rows")
        load_k(*keys_a)
        nc.scalar.dma_start(out=w_sb[:], in_=w.rearrange("(g p j) h -> p g (j h)", g=2, j=SLOTS))
        for first, vec in ((0, kg), (SLOTS, kb)):
            nc.scalar.dma_start(out=gain_rows[first:first + SLOTS, :].rearrange("j (b r) -> j b r", r=RUN),
                                in_=vec.rearrange("(b j r) -> j b r", j=SLOTS, r=RUN))
        load_k(*keys_b)
        load_wq(0)
        load_c(0)
        load_k(*keys_c)
        load_wq(1)
        load_wq(2)
        load_c(1)
        load_wq(3)

        ident = keep.tile([P, P], F32, name="ident")
        ident_bf = keep.tile([P, P], BF16, name="ident_bf")
        make_identity(nc, ident_bf[:])
        make_identity(nc, ident[:])
        w_col = keep.tile([P, 2, SLOTS * H], F32, name="w_col")
        gain_wide = keep.tile([P, P], F32, name="gain_wide")
        gain_col = keep.tile([P, 2 * SLOTS], F32, name="gain_col")
        nc.gpsimd.memset(gain_wide[:], 0.0)

        def gpsimd_copy(out, in_):
            nc.gpsimd.tensor_scalar(out, in_, 1.0, 1.0, ALU.mult, ALU.mult)

        def vector_copy(out, in_):
            nc.vector.tensor_copy(out=out, in_=in_)

        def scalar_copy(out, in_):
            nc.scalar.copy(out=out, in_=in_)

        def mx_tiles(name, width):
            codes = keep.tile([P, width], U32, name=name + "_codes", align_bytes=64)
            scales = keep.tile([P, width], U8, name=name + "_scales", align_bytes=64)
            return codes, scales

        def quantize(dst, cols, src):
            nc.vector.quantize_mx(out=dst[0][:, cols].bitcast(FP8X4), scales=dst[1][:, cols], in_=src)

        def mx_matmul(out, lhs, lhs_cols, rhs, rhs_cols):
            nc.tensor.matmul_mx(out=out, lhsT=lhs[0][:, lhs_cols].bitcast(FP8X4), lhsT_scale=lhs[1][:, lhs_cols],
                                rhs=rhs[0][:, rhs_cols].bitcast(FP8X4), rhs_scale=rhs[1][:, rhs_cols],
                                start=True, stop=True)

        def small_casts():
            nc.gpsimd.tensor_scalar(w_col[:], w_sb[:], SCORE_SCALE, 1.0, ALU.mult, ALU.mult)
            gpsimd_copy(gain_wide[0:2 * SLOTS, :], gain_rows[:])

        def gains_to_partitions():
            bank = scalar_bank()
            nc.tensor.transpose(bank[:, 0:P], gain_wide[:], ident[:])
            scalar_copy(gain_col[:], bank[:, 0:2 * SLOTS])

        kn_mx = mx_tiles("kn", T)
        stats, mean_var, rstd, normed, kn_slots, kn_words = {}, {}, {}, {}, {}, {}

        def key_stats(*tiles):
            for n in tiles:
                stats[n] = keep.tile([P, 6], F32, name="stats%d" % n)
                nc.vector.bn_stats(stats[n][:], k_sb[n])

        def key_moments(first, count, order):
            mean_var[first] = keep.tile([P, count, 2], F32, name="mean_var%d" % first)
            for n in order:
                nc.vector.bn_aggr(mean_var[first][:, n, :], stats[first + n][:])

        def key_rstd(first, count):
            rstd[first] = keep.tile([P, count], F32, name="rstd%d" % first)
            nc.scalar.activation(rstd[first][:], mean_var[first][:, :, 1], ACT.Abs_reciprocal_sqrt, bias=EPS)

        def key_normalize(first, count):
            for n in range(count):
                normed[first + n] = work.tile([P, SLOTS, P], F32, name="normed", bufs=4)
                nc.vector.tensor_scalar(normed[first + n][:].rearrange("t j (b r) -> t j b r", r=RUN),
                                        k_sb[first + n].rearrange("t (b j r) -> t j b r", j=SLOTS, r=RUN),
                                        mean_var[first][:, n, 0:1], rstd[first][:, n:n + 1], ALU.subtract, ALU.mult)

        def key_turn(half):
            kn_slots[half] = work.tile([P, SLOTS, BANK], BF16, name="kn_slots", bufs=1)
            for j in range(SLOTS):
                bank = scalar_bank()
                for n in range(4):
                    nc.tensor.transpose(bank[:, blk(n)], normed[4 * half + n][:, j, :], ident[:])
                nc.scalar.activation(kn_slots[half][:, j, :], bank[:], ACT.Identity,
                                     bias=gain_col[:, SLOTS + j:SLOTS + j + 1], scale=gain_col[:, j:j + 1])

        def key_pack(half):
            kn_words[half] = work.tile([P, BANK, SLOTS], BF16, name="kn_words", bufs=1, align_bytes=64)
            vector_copy(kn_words[half][:].rearrange("p (m e) j -> p m j e", e=4),
                        kn_slots[half][:].rearrange("p j (m e) -> p m j e", e=4))

        def key_quantize(half):
            quantize(kn_mx, blk(half, BANK), kn_words[half][:].rearrange("p t j -> p (t j)"))

        c_mx, c_words, wq_mx, wq_words = {}, {}, {}, {}

        def c_turn(g):
            words = c_sb[g][:].rearrange("p j i -> p (j i)").bitcast(F32)
            c_words[g] = work.tile([P, BANK * SLOTS], BF16, name="c_words", bufs=1, align_bytes=64)
            for pair in range(2):
                bank = scalar_bank()
                for jj in range(2):
                    j = 2 * pair + jj
                    for u in range(2):
                        nc.tensor.transpose(bank[:, blk(2 * jj + u)], words[:, j * 256 + u:(j + 1) * 256:2], ident[:])
                scalar_copy(c_words[g][:, blk(pair, 1024)].bitcast(F32).rearrange("p (jj r u) -> p jj r u", jj=2, u=2),
                            bank[:].rearrange("p (jj u r) -> p jj r u", jj=2, u=2))

        def c_quantize(g):
            c_mx[g] = mx_tiles("c%d" % g, BANK)
            quantize(c_mx[g], slice(0, BANK), c_words[g][:])

        def wq_pack(h, first, count, copy, stage):
            wq_words[h, first] = work.tile([P, count, P, SLOTS], BF16, name=stage, bufs=1, align_bytes=64)
            for j in range(first, first + count):
                dst = wq_words[h, first][:, j - first, :, :]
                if copy is gpsimd_copy:
                    src = wq_sb[h][:].rearrange("p i (b j r) -> p j b r i", j=SLOTS, r=RUN)
                    copy(dst.rearrange("p (b r) i -> p b r i", r=RUN), src[:, j, :, :, :])
                else:
                    src = wq_sb[h][:].rearrange("p i (b j u e) -> p j b u i e", j=SLOTS, u=2, e=4)
                    copy(dst.rearrange("p (b u e) i -> p b u i e", u=2, e=4), src[:, j, :, :, :, :])

        def wq_quantize(h, first, count):
            if h not in wq_mx:
                wq_mx[h] = mx_tiles("wq%d" % h, D)
            quantize(wq_mx[h], slice(first * P, (first + count) * P),
                     wq_words[h, first][:].rearrange("p j m i -> p (j m i)"))

        q_mx, q_words = {}, {}

        def queries(g, h, slots=range(SLOTS)):
            for slot in slots:
                bank = scalar_bank()
                for j in range(SLOTS):
                    mx_matmul(bank[:, blk(j)], wq_mx[h], blk(j), c_mx[g], blk(slot))
                if slot == 0:
                    q_words[g, h] = work.tile([P, BANK, SLOTS], BF16, name="q_words", bufs=3, align_bytes=64)
                    q_mx[g, h] = mx_tiles("q%d%d" % (g, h), BANK)
                scalar_copy(q_words[g, h][:, blk(slot), :], bank[:].rearrange("p (j n) -> p n j", j=SLOTS))

        def query_quantize(g, h):
            quantize(q_mx[g, h], slice(0, BANK), q_words[g, h][:].rearrange("p s j -> p (s j)"))

        w_row, w_bank = {}, {}

        def weight_spread(g, h):
            w_bank[g, h] = vector_bank()
            for j in range(SLOTS):
                col = w_sb[:, g, j * H + h:j * H + h + 1]
                nc.tensor.matmul(w_bank[g, h][:, blk(j)], lhsT=col.to_broadcast([P, P]), rhs=ident_bf[:],
                                 start=True, stop=True)

        def weight_row(g, h):
            w_row[g, h] = keep.tile([P, BANK], F32, name="w_row%d%d" % (g, h))
            nc.scalar.activation(w_row[g, h][:], w_bank[g, h][:], ACT.Copy, scale=SCORE_SCALE)

        km_bank, km_term, qm_bank, qm_relu, sum_bank, partial, result = {}, {}, {}, {}, {}, {}, {}
        result_words, result_codes, result_scales = {}, {}, {}

        def km_matmul(quarter, h, *tiles):
            g, half = divmod(quarter, 2)
            for n in tiles:
                km_bank[quarter, h, n] = vector_bank()
                mx_matmul(km_bank[quarter, h, n][:], kn_mx, blk(4 * half + n), q_mx[g, h], slice(0, BANK))

        def km_weigh(quarter, h, *tiles):
            for n in tiles:
                km_term[quarter, h, n] = work.tile([P, BANK], F32, name="km_term", bufs=24)
                nc.vector.scalar_tensor_tensor(km_term[quarter, h, n][:], km_bank[quarter, h, n][:], 0.0,
                                               w_row[quarter // 2, h][:], ALU.max, ALU.mult)

        def qm_matmul(quarter, slot, h):
            g, half = divmod(quarter, 2)
            qm_bank[quarter, slot, h] = scalar_bank()
            mx_matmul(qm_bank[quarter, slot, h][:], q_mx[g, h], blk(slot), kn_mx, blk(half, BANK))

        def qm_clip(quarter, slot, h):
            qm_relu[quarter, slot, h] = work.tile([P, BANK], F32, name="qm_relu", bufs=2 * (MAX_LEAD + 2))
            nc.scalar.activation(qm_relu[quarter, slot, h][:], qm_bank[quarter, slot, h][:], ACT.Relu)

        def sum_turn(quarter, slot):
            sum_bank[quarter, slot] = vector_bank()
            for n in range(4):
                for h in range(2):
                    nc.tensor.matmul(sum_bank[quarter, slot][:, blk(n)], lhsT=km_term[quarter, h, n][:, blk(slot)],
                                     rhs=ident[:], start=(h == 0), stop=(h == 1), is_transpose=True)

        def weight(quarter, slot, h):
            return w_col[:, quarter // 2, slot * H + h:slot * H + h + 1]

        def add_head2(quarter, slot):
            partial[quarter, slot] = work.tile([P, BANK], F32, name="partial", bufs=3)
            nc.vector.scalar_tensor_tensor(partial[quarter, slot][:], qm_relu[quarter, slot, 2][:],
                                           weight(quarter, slot, 2), sum_bank[quarter, slot][:], ALU.mult, ALU.add)

        def add_head3(quarter, slot, cols=slice(0, BANK)):
            g, half = divmod(quarter, 2)
            if slot == 0:
                result[quarter] = work.tile([P, SLOTS, BANK], F32, name="result", tag="wq_then_result", bufs=4)
            nc.vector.scalar_tensor_tensor(result[quarter][:, slot, cols], qm_relu[quarter, slot, 3][:, cols],
                                           weight(quarter, slot, 3), partial[quarter, slot][:, cols], ALU.mult, ALU.add)
            rows = out_0[blk(g, BANK), blk(half, BANK)].rearrange("(p j) t -> p j t", j=SLOTS)
            nc.sync.dma_start(out=rows[:, slot, cols], in_=result[quarter][:, slot, cols])

        def result_pack(quarter, first, count, copy, stage):
            result_words[quarter, first] = work.tile([P, count * P, SLOTS], BF16, name=stage, align_bytes=64)
            src = result[quarter][:, :, first * P:(first + count) * P]
            if copy is gpsimd_copy:
                copy(result_words[quarter, first][:], src.rearrange("p j t -> p t j"))
            else:
                copy(result_words[quarter, first][:].rearrange("p (m e) j -> p m j e", e=4),
                     src.rearrange("p j (m e) -> p m j e", e=4))

        def result_quantize(quarter, first, count):
            g, half = divmod(quarter, 2)
            if quarter not in result_codes:
                result_codes[quarter] = work.tile([P, BANK], U32, name="result_codes", align_bytes=64)
            if g not in result_scales:
                result_scales[g] = keep.tile([P, T], U8, name="result_scales%d" % g, align_bytes=64)
            cols = slice(first * P, (first + count) * P)
            nc.vector.quantize_mx(out=result_codes[quarter][:, cols].bitcast(FP8X4),
                                  scales=result_scales[g][:, half * BANK + cols.start:half * BANK + cols.stop],
                                  in_=result_words[quarter, first][:].rearrange("p t j -> p (t j)"))

        def store_codes(quarter, cols=slice(0, BANK)):
            g, half = divmod(quarter, 2)
            dst = out_1[g].rearrange("p m t -> p (m t)").bitcast(I32)[:, blk(half, BANK)]
            nc.sync.dma_start(out=dst[:, cols], in_=result_codes[quarter][:, cols].bitcast(I32))

        def store_scales(g, queues):
            for q in range(4):
                queues[q % len(queues)].dma_start(out=out_2[g, 4 * q:4 * q + 4, :].bitcast(I32),
                                                  in_=result_scales[g][32 * q:32 * q + 4, :].bitcast(I32))

        key_stats(0, 1, 2)
        small_casts()
        key_moments(*keys_a, (1, 0))
        key_rstd(*keys_a)
        for g in range(2):
            for h in range(2):
                weight_spread(g, h)
        wq_pack(0, 2, 2, scalar_copy, "engine_stage")
        key_stats(3)
        key_normalize(*keys_a)
        key_moments(*keys_b, (1, 0))
        key_rstd(*keys_b)
        gains_to_partitions()
        wq_pack(0, 0, 2, vector_copy, "gpsimd_stage")
        weight_row(0, 0)
        c_turn(0)
        weight_row(0, 1)
        key_normalize(*keys_b)
        wq_quantize(0, 2, 2)
        key_stats(4)
        c_quantize(0)
        wq_quantize(0, 0, 2)
        key_turn(0)
        queries(0, 0)

        wq_pack(1, 0, 2, gpsimd_copy, "gpsimd_stage")
        key_stats(5, 6, 7)
        key_moments(*keys_c, (2, 0, 1, 3))
        key_rstd(*keys_c)
        key_pack(0)
        wq_pack(1, 2, 2, vector_copy, "engine_stage")
        weight_row(1, 0)
        weight_row(1, 1)
        c_turn(1)
        wq_pack(2, 2, 2, scalar_copy, "wq2_stage")
        key_quantize(0)
        query_quantize(0, 0)
        km_matmul(0, 0, 0, 1, 2, 3)
        key_normalize(*keys_c)
        key_turn(1)
        wq_quantize(1, 2, 2)
        c_quantize(1)
        wq_quantize(1, 0, 2)

        wq_pack(2, 0, 2, gpsimd_copy, "gpsimd_stage")
        queries(0, 1)
        wq_pack(3, 3, 1, scalar_copy, "wq3_stage")
        km_weigh(0, 0, 3, 2, 1, 0)
        queries(1, 0)
        key_pack(1)
        wq_quantize(2, 2, 2)
        key_quantize(1)
        query_quantize(0, 1)
        km_matmul(0, 1, 0, 1, 2, 3)
        wq_quantize(3, 3, 1)
        wq_quantize(2, 0, 2)
        wq_pack(3, 0, 3, gpsimd_copy, "gpsimd_stage")
        queries(0, 2, (0, 1))
        km_weigh(0, 1, 0, 1)
        km_matmul(1, 0, 0, 1)
        queries(0, 2, (2, 3))
        km_weigh(0, 1, 3, 2)
        km_matmul(1, 0, 2, 3)
        km_weigh(1, 0, 1)
        wq_quantize(3, 0, 3)
        queries(0, 3)
        query_quantize(1, 0)
        km_weigh(1, 0, 0)
        km_matmul(1, 1, 0, 1)
        query_quantize(0, 2)
        km_weigh(1, 0, 3, 2)

        group1_queries = [(h, slot) for h in (1, 2, 3) for slot in range(SLOTS)]
        group1_products = [(quarter, h, n) for h in range(2) for quarter in (2, 3) for n in range(4)]

        def scalar_work(u):
            quarter, slot = UNITS[u]
            for h, query_slot in group1_queries[2 * u:2 * u + 2]:
                queries(1, h, (query_slot,))
            qm_matmul(quarter, slot, 3)
            qm_matmul(quarter, slot, 2)
            qm_clip(quarter, slot, 2)
            qm_clip(quarter, slot, 3)

        qm_matmul(0, 0, 2)
        qm_clip(0, 0, 2)
        queries(1, 1, (0, 1))
        km_matmul(1, 1, 2, 3)
        km_weigh(1, 1, 0)
        sum_turn(0, 0)
        query_quantize(0, 3)
        qm_matmul(0, 0, 3)
        qm_clip(0, 0, 3)
        scalar_work(1)
        km_weigh(1, 1, 1, 3, 2)

        issued = 2
        taken = 0
        for step, (quarter, slot) in enumerate(UNITS[:-1]):
            products = group1_products[taken:taken + (2 if step < DOUBLE_STEPS else 1)]
            taken = taken + len(products)
            for product in products:
                km_matmul(*product)
            lead = min(MAX_LEAD, max(1, step - QUERY_UNITS + 2))
            while issued <= min(step + lead, len(UNITS) - 1):
                scalar_work(issued)
                issued = issued + 1
            for product in products[:1]:
                km_weigh(*product)
            add_head2(quarter, slot)
            for product in products[1:]:
                km_weigh(*product)
            sum_turn(*UNITS[step + 1])
            if step > 0:
                add_head3(*UNITS[step - 1])
            if step < QUERY_UNITS and step % 2 == 1:
                query_quantize(1, step // 2 + 1)
            late, part = divmod(step - 5, 4)
            if 7 <= step <= 10:
                result_quantize(0, step - 7, 1)
            if step == 10:
                store_codes(0)
            if late == 0:
                result_pack(0, part, 1, gpsimd_copy, "gpsimd_result")
            if late > 0 and part < 2:
                result_pack(late, 2 * part, 2, scalar_copy, "scalar_result")
            if late == 1 and part >= 2:
                result_quantize(1, 2 * (part - 2), 2)
            if step == 12:
                store_codes(1)
                store_scales(0, [nc.sync])

        low, high = slice(0, BANK // 2), slice(BANK // 2, BANK)
        add_head2(3, 3)
        add_head3(3, 2)
        add_head3(3, 3, low)
        result_pack(3, 0, 2, scalar_copy, "last_low")
        add_head3(3, 3, high)
        result_quantize(2, 0, 2)
        result_pack(3, 2, 2, vector_copy, "last_high")
        result_quantize(2, 2, 2)
        store_codes(2)
        result_quantize(3, 2, 2)
        store_codes(3, high)
        result_quantize(3, 0, 2)
        store_codes(3, low)
        store_scales(1, [nc.sync, nc.scalar])
